import numpy as np
import ml_dtypes


def mxq(x, axis, fmt="e4m3"):
    dtype, down = {"e4m3": (ml_dtypes.float8_e4m3fn, 7), "e5m2": (ml_dtypes.float8_e5m2, 14)}[fmt]
    v = np.moveaxis(np.asarray(x, np.float32).astype(ml_dtypes.bfloat16).astype(np.float64), axis, -1)
    blocks = v.reshape(v.shape[:-1] + (-1, 32))
    amax = np.abs(blocks).max(-1, keepdims=True)
    byte = np.maximum(np.where(amax > 0, np.frexp(amax)[1] - 1 + 127, 0) - down, 1)
    scale = np.exp2(byte - 127.0)
    codes = (blocks / scale).astype(np.float32).astype(dtype).astype(np.float64)
    return np.moveaxis((codes * scale).reshape(v.shape), -1, axis)


WIDE = False


def mx_kscale(k):
    if not WIDE:
        return np.ones(k)
    levels = np.array([10, -10, 5, -5, 0])
    if k % 512:
        return np.exp2(np.random.permutation(np.resize(levels, k // 32))).repeat(32)
    a = np.empty((k // 512, 16))
    for p in range(k // 512):
        a[p, :8] = np.random.permutation(np.resize(levels, 8))
        for g in range(8):
            far = levels[np.abs(levels - a[p, g]) >= 10]
            a[p, g + 8] = far[np.random.randint(len(far))]
    return np.exp2(a.ravel()).repeat(32)


def f64(x):
    return np.asarray(x).astype(np.float64)


def striped(idx):
    return np.tile(idx.reshape(-1, 16).T, (8, 1)).astype(np.uint16)


def unstriped(offs):
    return offs[:16].T.reshape(-1).astype(np.int64)


E2M1 = np.array([0.0, 0.5, 1.0, 1.5, 2.0, 3.0, 4.0, 6.0, -0.0, -0.5, -1.0, -1.5, -2.0, -3.0, -4.0, -6.0])


def pack_weight(w, fmt):
    k, n = w.shape
    w = f64(np.asarray(w, np.float32).astype(ml_dtypes.bfloat16)).reshape(k // 32, 32, n)
    amax = np.abs(w).max(1)
    if fmt == "e4m3":
        byte = np.frexp(amax)[1] - 1 + 127 - 7
    else:
        mant, ex = np.frexp(amax / 6.0)
        byte = np.where(mant > 0.5, ex, ex - 1) + 127
    byte = np.clip(np.where(amax > 0, byte, 1), 1, 254)
    scaled = (w * np.exp2(127.0 - byte)[:, None, :]).reshape(k, n).astype(np.float32)
    by_word = np.ascontiguousarray(scaled.reshape(k // 512, 128, 4, n).transpose(0, 1, 3, 2))
    if fmt == "e4m3":
        words = by_word.astype(ml_dtypes.float8_e4m3fn).view(np.uint8)
    else:
        c = by_word.astype(ml_dtypes.float4_e2m1fn).view(np.uint8) & 0xF
        words = (c[..., 0::2] | (c[..., 1::2] << 4)).reshape(k // 512, 128, 2 * n)
    return np.ascontiguousarray(words), np.ascontiguousarray(byte.astype(np.uint8).reshape(k // 512, 16, n))


def unpack_weight(words, scales, fmt):
    g, _, n = scales.shape
    words = np.ascontiguousarray(words).reshape(g, 128, n, -1)
    if fmt == "e4m3":
        vals = words.view(ml_dtypes.float8_e4m3fn).astype(np.float64)
    else:
        nib = np.empty((g, 128, n, 4), np.uint8)
        nib[..., 0::2] = words & 0xF
        nib[..., 1::2] = words >> 4
        vals = E2M1[nib]
    vals = vals * np.repeat(np.exp2(scales.astype(np.float64) - 127.0), 8, axis=1)[..., None]
    return vals.transpose(0, 1, 3, 2).reshape(g * 512, n)


def gelu(v):
    return 0.5 * v * (1.0 + np.tanh(np.sqrt(2.0 / np.pi) * (v + 0.044715 * v**3)))


K, H, N, T, S, P = 1024, 1024, 512, 2048, 1024, 512

def setup_inputs():
    n = np.random.standard_normal
    s = mx_kscale(K)[:, None]
    u = mx_kscale(H)[:, None]
    tab_words, tab_scales = pack_weight(n((K, T)) * s, "e4m3")
    w2_words, w2_scales = pack_weight(n((K, H)) / s / np.sqrt(K), "e2m1")
    w4_words, w4_scales = pack_weight(0.4 * n((H, N)) / u / np.sqrt(H), "e4m3")
    return {
        "tab_words": tab_words, "tab_scales": tab_scales,
        "offs": striped(np.random.permutation(T)[:S]),
        "pos1": striped(np.random.permutation(S)[:P]),
        "pos2": striped(np.random.permutation(S)[:P]),
        "pos3": striped(np.random.permutation(S)[:P]),
        "w1": (n((K, H)) / s / np.sqrt(K) * u.T).astype(np.float32),
        "w2_words": w2_words, "w2_scales": w2_scales,
        "w4_words": w4_words, "w4_scales": w4_scales,
        "target": (0.6 * n((N, P))).astype(np.float32),
    }

def reference(tab_words, tab_scales, offs, pos1, pos2, pos3, w1,
              w2_words, w2_scales, w4_words, w4_scales, target):
    v = unpack_weight(tab_words, tab_scales, "e4m3")[:, unstriped(offs)]
    w2 = unpack_weight(w2_words, w2_scales, "e2m1")
    w4 = unpack_weight(w4_words, w4_scales, "e4m3")
    h = mxq(f64(w1), 0, "e4m3").T @ v
    e = w2.T @ v
    dock = h[:, unstriped(pos1)]
    tour = e[:, unstriped(pos2)]
    sail = h[:, unstriped(pos3)]
    z = np.abs(dock) + tour * sail
    y = w4.T @ mxq(z, 0, "e4m3")
    res = f64(target) - y
    return np.square(res) * res

@@ -1,0 +1,307 @@
+from contextlib import ExitStack
+
+import concourse.mybir as mybir
+from concourse.masks import make_identity
+
+K, H, N, T, S, M = 1024, 1024, 512, 2048, 1024, 512
+FLOPS = 2 * K * H * S * 2 + 2 * H * N * M
+
+F32 = mybir.dt.float32
+BF16 = mybir.dt.bfloat16
+I32 = mybir.dt.int32
+U32 = mybir.dt.uint32
+U16 = mybir.dt.uint16
+U8 = mybir.dt.uint8
+E4M3 = mybir.dt.float8_e4m3fn_x4
+E2M1 = mybir.dt.float4_e2m1fn_x4
+ACT = mybir.ActivationFunctionType
+ALU = mybir.AluOpType
+
+P = 128
+PACK = 4
+PASS = P * PACK
+BANK = 512
+QUADS = 4
+R_TILES = H // P
+M_TILES = M // P
+N_TILES = N // P
+TILES_PER_PASS = PASS // P
+W1_CHUNKS = [128, 128, 256, 256, 256]
+
+
+def tile_list_cruise_slot_corrections_kernel(
+    tc, tab_words, tab_scales, offs, pos1, pos2, pos3, w1, w2_words, w2_scales, w4_words, w4_scales, target, out
+):
+    nc = tc.nc
+    with ExitStack() as ctx:
+        keep = ctx.enter_context(tc.tile_pool(name="keep", bufs=1))
+        w1_ring = ctx.enter_context(tc.tile_pool(name="w1_ring", bufs=4))
+        windows = ctx.enter_context(tc.tile_pool(name="windows", bufs=3))
+        picks = ctx.enter_context(tc.tile_pool(name="picks", bufs=3))
+        tail = ctx.enter_context(tc.tile_pool(name="tail", bufs=4))
+        ends = ctx.enter_context(tc.tile_pool(name="ends", bufs=4))
+        sums = ctx.enter_context(tc.psum_pool(name="sums", bufs=5))
+        turns = ctx.enter_context(tc.psum_pool(name="turns", bufs=2))
+
+        offs_sb = keep.tile([P, S // 16], U16, name="offs_sb")
+        pos_sb = [keep.tile([P, M // 16], U16, name=f"pos{i + 1}_sb") for i in range(3)]
+
+        tab_sc = keep.tile([P, T], U8, name="tab_sc", tag="tab_sc", align_bytes=64)
+        nc.gpsimd.memset(tab_sc[:].bitcast(I32), 0)
+        v_sc1 = keep.tile([P, S], U8, name="v_sc1", align_bytes=64)
+        w2_sc = keep.tile([P, 2, H], U8, name="w2_sc", align_bytes=64)
+        nc.vector.memset(w2_sc[:].rearrange("p a c -> p (a c)").bitcast(I32), 0)
+        nc.vector.memset(v_sc1[:].bitcast(I32), 0)
+        w4_sc = keep.tile([P, 2, N], U8, name="w4_sc", align_bytes=64)
+        nc.vector.memset(w4_sc[:].rearrange("p a c -> p (a c)").bitcast(I32), 0)
+        ident = keep.tile([P, P], F32, name="ident")
+        make_identity(nc, ident[:])
+        for q in range(QUADS):
+            nc.gpsimd.dma_start(
+                w2_sc[32 * q : 32 * q + 4, :, :].bitcast(I32),
+                w2_scales[:, 4 * q : 4 * q + 4, :].rearrange("a r c -> r a c").bitcast(I32),
+            )
+        for q in range(QUADS):
+            nc.gpsimd.dma_start(
+                w4_sc[32 * q : 32 * q + 4, :, :].bitcast(I32),
+                w4_scales[:, 4 * q : 4 * q + 4, :].rearrange("a r c -> r a c").bitcast(I32),
+            )
+
+        tab_w = [keep.tile([P, T], I32, name=f"tab_w{a}", tag=f"tab_w{a}", align_bytes=64) for a in range(2)]
+
+        chunk_start = [sum(W1_CHUNKS[:c]) for c in range(len(W1_CHUNKS))]
+        w1_raw = {}
+
+        def load_w1(c):
+            cols = slice(chunk_start[c], chunk_start[c] + W1_CHUNKS[c])
+            for a in range(2):
+                raw = w1_ring.tile([P, PACK, W1_CHUNKS[c]], F32, name="w1_raw", tag="w1_raw", align_bytes=64)
+                nc.sync.dma_start(raw[:], w1[a * PASS : (a + 1) * PASS, cols].rearrange("(p j) c -> p j c", j=PACK))
+                w1_raw[c, a] = raw
+
+        nc.sync.dma_start(offs_sb[:], offs)
+        for sb, pos in zip(pos_sb, (pos1, pos2, pos3)):
+            nc.sync.dma_start(sb[:], pos)
+        nc.sync.dma_start(tab_w[0][:], tab_words[0].rearrange("p t i -> p (t i)").bitcast(I32))
+        for q in range(QUADS):
+            nc.scalar.dma_start(tab_sc[32 * q : 32 * q + 8, :].bitcast(I32), tab_scales[:, 4 * q : 4 * q + 4, :].bitcast(I32))
+        load_w1(0)
+        nc.sync.dma_start(tab_w[1][:], tab_words[1].rearrange("p t i -> p (t i)").bitcast(I32))
+        load_w1(1)
+        w2_w = keep.tile([P, 2, 2 * H], U8, name="w2_w", align_bytes=64)
+        nc.sync.dma_start(w2_w[:].bitcast(I32), w2_words.rearrange("a p c -> p a c").bitcast(I32))
+
+        v_sc = keep.tile([P, S], U8, name="v_sc", align_bytes=64)
+        v_words = keep.tile([P, 2 * S], U32, name="v_words", tag="tab_sc", align_bytes=64)
+        v_w = {}
+
+        def gather_words(a):
+            for half in range(S // BANK):
+                lst = offs_sb[:, half * (BANK // 16) : (half + 1) * (BANK // 16)]
+                words = v_words[:, a * S + half * BANK : a * S + (half + 1) * BANK]
+                nc.vector.tensor_copy(words, tab_w[a][:].bitcast(U32).indirect(lst))
+                v_w[half, a] = words
+
+        nc.vector.tensor_copy(v_sc[:], tab_sc[:].indirect(offs_sb[:]))
+        for q in range(QUADS):
+            nc.scalar.dma_start(v_sc1[32 * q : 32 * q + 4, :].bitcast(I32), v_sc[32 * q + 4 : 32 * q + 8, :].bitcast(I32))
+        gather_words(0)
+        gather_words(1)
+
+        w1_codes, w1_sc = {}, {}
+
+        def quantise_w1(c):
+            width = W1_CHUNKS[c]
+            for a in range(2):
+                grouped = w1_ring.tile([P, width, PACK], BF16, name="w1_grouped", align_bytes=64)
+                nc.scalar.copy(
+                    grouped[:].rearrange("p (c i) j -> p c j i", i=4),
+                    w1_raw[c, a][:].rearrange("p j (c i) -> p c j i", i=4),
+                )
+                codes = keep.tile([P, width], U32, name=f"w1_codes{c}{a}", align_bytes=64)
+                scales = keep.tile([P, width], U8, name=f"w1_sc{c}{a}", align_bytes=64)
+                nc.vector.quantize_mx(
+                    out=codes[:].bitcast(E4M3), scales=scales[:], in_=grouped[:].rearrange("p c j -> p (c j)")
+                )
+                for rt in range(chunk_start[c] // P, (chunk_start[c] + width) // P):
+                    cols = slice(rt * P - chunk_start[c], (rt + 1) * P - chunk_start[c])
+                    w1_codes[rt, a] = codes[:, cols]
+                    w1_sc[rt, a] = scales[:, cols]
+
+        h_win, e_win = {}, {}
+
+        def features(rt):
+            h = windows.tile([P, S], F32, name="h")
+            e = windows.tile([P, S], F32, name="e")
+            def berth(half, a):
+                return w1_codes[rt, a].bitcast(E4M3), w1_sc[rt, a], v_sc[4 * a :, half * BANK : (half + 1) * BANK]
+
+            def excursion(half, a):
+                return (
+                    w2_w[:, a, 2 * P * rt : 2 * P * (rt + 1)].bitcast(E2M1),
+                    w2_sc[:, a, P * rt : P * (rt + 1)],
+                    (v_sc, v_sc1)[a][:, half * BANK : (half + 1) * BANK],
+                )
+
+            jobs = [(h, berth), (e, excursion)]
+            for window, operands in jobs if rt < R_TILES - 1 else reversed(jobs):
+                for half in range(S // BANK):
+                    acc = sums.tile([P, BANK], F32, name="acc")
+                    for a in range(2):
+                        weights, weight_sc, moving_sc = operands(half, a)
+                        nc.tensor.matmul_mx(
+                            out=acc[:],
+                            lhsT=weights,
+                            lhsT_scale=weight_sc,
+                            rhs=v_w[half, a].bitcast(E4M3),
+                            rhs_scale=moving_sc,
+                            start=(a == 0),
+                            stop=(a == 1),
+                        )
+                    nc.scalar.copy(window[:, half * BANK : (half + 1) * BANK], acc[:])
+            h_win[rt], e_win[rt] = h, e
+
+        dock_abs, prod = {}, {}
+
+        def places(which, mts):
+            return pos_sb[which][:, mts[0] * (P // 16) : (mts[-1] + 1) * (P // 16)]
+
+        def pick_dock(rt):
+            dock = picks.tile([P, M], F32, name="dock")
+            da = picks.tile([P, M], F32, name="dock_abs")
+            nc.vector.tensor_copy(dock[:], h_win[rt][:].indirect(pos_sb[0][:]))
+            nc.scalar.activation(da[:], dock[:], ACT.Abs)
+            for mt in range(M_TILES):
+                dock_abs[rt, mt] = da[:, mt * P : (mt + 1) * P]
+
+        def pick_sail(rt, mts, pool):
+            sail = pool.tile([P, len(mts) * P], F32, name="sail")
+            nc.vector.tensor_copy(sail[:], h_win[rt][:].indirect(places(2, mts)))
+            return sail
+
+        def pick_tour(rt, mts, pool, sail):
+            pr = pool.tile([P, len(mts) * P], F32, name="prod")
+            nc.vector.tensor_tensor(pr[:], e_win[rt][:].indirect(places(1, mts)), sail[:], ALU.mult)
+            for i, mt in enumerate(mts):
+                prod[rt, mt] = pr[:, i * P : (i + 1) * P]
+
+        z_t = [keep.tile([P, M_TILES * PASS], BF16, name=f"z_t{b}", align_bytes=64) for b in range(2)]
+
+        def add_turned(rt, mts, spare=False):
+            b, j = divmod(rt, TILES_PER_PASS)
+            if spare:
+                turned = sums.tile([P, len(mts), P], F32, name="acc")
+            else:
+                turned = turns.tile([P, len(mts), P], F32, name="turned", bufs=1)
+            for i, mt in enumerate(mts):
+                nc.tensor.matmul(turned[:, i, :], prod[rt, mt], ident[:], start=True, stop=False, is_transpose=True)
+                nc.tensor.matmul(turned[:, i, :], dock_abs[rt, mt], ident[:], start=False, stop=True, is_transpose=True)
+            dst = z_t[b][:, mts[0] * PASS : (mts[-1] + 1) * PASS].rearrange(
+                "p (t u j q e) -> p t u j q e", u=2, j=TILES_PER_PASS, q=32, e=2
+            )[:, :, :, j, :, :]
+            nc.scalar.copy(dst, turned[:].rearrange("p t (q u e) -> p t u q e", u=2, e=2))
+
+        z_codes = [keep.tile([P, M], U32, name=f"z_codes{b}", align_bytes=64) for b in range(2)]
+        z_sc = [keep.tile([P, M], U8, name=f"z_sc{b}", align_bytes=64) for b in range(2)]
+
+        def quantise_z(b, mts):
+            back = turns.tile([P, len(mts), 2, P], F32, name="back")
+            for i, mt in enumerate(mts):
+                words = z_t[b][:, mt * PASS : (mt + 1) * PASS].bitcast(F32)
+                for u in range(2):
+                    nc.tensor.transpose(back[:, i, u, :], words[:, u * P : (u + 1) * P], ident[:])
+            grouped = picks.tile([P, len(mts) * PASS], BF16, name="z_grouped", align_bytes=64)
+            nc.scalar.copy(
+                grouped[:].bitcast(F32).rearrange("p (t m u) -> p t m u", t=len(mts), u=2),
+                back[:].rearrange("p t u m -> p t m u"),
+            )
+            cols = slice(mts[0] * P, (mts[-1] + 1) * P)
+            nc.vector.quantize_mx(out=z_codes[b][:, cols].bitcast(E4M3), scales=z_sc[b][:, cols], in_=grouped[:])
+
+        second = {}
+
+        def load_second_stage():
+            w4_w = w1_ring.tile([P, 2, N], I32, name="w4_w", tag="w1_raw", align_bytes=64)
+            second["w4_w"] = w4_w
+            nc.sync.dma_start(w4_w[:], w4_words.rearrange("a p c i -> p a (c i)").bitcast(I32))
+            for half in range(2):
+                part = w1_ring.tile([P, N_TILES, M // 2], F32, name="target_sb", tag="w1_raw", align_bytes=64)
+                cols = slice(half * (M // 2), (half + 1) * (M // 2))
+                nc.sync.dma_start(part[:], target.rearrange("(t p) m -> p t m", p=P)[:, :, cols])
+                for i in range(2):
+                    second[2 * half + i] = part[:, :, i * P : (i + 1) * P]
+
+        def scores(y, b, mt):
+            cols = slice(mt * P, (mt + 1) * P)
+            for nt in range(N_TILES):
+                nc.tensor.matmul_mx(
+                    out=y[:, nt, :],
+                    lhsT=second["w4_w"][:, b, nt * P : (nt + 1) * P].bitcast(E4M3),
+                    lhsT_scale=w4_sc[:, b, nt * P : (nt + 1) * P],
+                    rhs=z_codes[b][:, cols].bitcast(E4M3),
+                    rhs_scale=z_sc[b][:, cols],
+                    start=(b == 0 and nt == 0),
+                    stop=(b == 1 and nt == N_TILES - 1),
+                )
+
+        def finish(y, mt):
+            cols = slice(mt * P, (mt + 1) * P)
+            res = ends.tile([P, N_TILES, P], F32, name="res")
+            sq = ends.tile([P, N_TILES, P], F32, name="sq")
+            cube = ends.tile([P, N_TILES, P], F32, name="cube", bufs=4)
+            nc.vector.tensor_tensor(res[:], second[mt], y[:], ALU.subtract)
+            nc.scalar.activation(sq[:], res[:], ACT.Square)
+            nc.vector.tensor_tensor(cube[:], sq[:], res[:], ALU.mult)
+            nc.sync.dma_start(out.rearrange("(t p) m -> p t m", p=P)[:, :, cols], cube[:])
+
+        all_mts = list(range(M_TILES))
+        last = R_TILES - 1
+        chunk_of = {chunk_start[c] // P: c for c in range(len(W1_CHUNKS))}
+
+        def prepare(rt):
+            if rt in chunk_of:
+                c = chunk_of[rt]
+                quantise_w1(c)
+                if c + 2 < len(W1_CHUNKS):
+                    load_w1(c + 2)
+                if c + 2 == len(W1_CHUNKS) - 1:
+                    load_second_stage()
+
+        prepare(0)
+        prepare(1)
+        features(0)
+        prepare(2)
+        features(1)
+        prepare(4)
+        for rt in range(last):
+            sail = pick_sail(rt, all_mts, picks)
+            pick_dock(rt)
+            pick_tour(rt, all_mts, picks, sail)
+            if rt >= 1:
+                add_turned(rt - 1, all_mts)
+            if rt == TILES_PER_PASS:
+                quantise_z(0, [0, 1])
+                quantise_z(0, [2, 3])
+            if rt + 2 < R_TILES:
+                features(rt + 2)
+            if rt == 1:
+                prepare(6)
+        add_turned(last - 1, all_mts)
+        ys = [sums.tile([P, N_TILES, P], F32, name="acc") for mt in all_mts]
+        pick_dock(last)
+        sails = [pick_sail(last, [0], tail)]
+        for mt in all_mts:
+            if mt + 1 < M_TILES:
+                sails.append(pick_sail(last, [mt + 1], tail))
+            pick_tour(last, [mt], tail, sails[mt])
+        for mt in all_mts:
+            scores(ys[mt], 0, mt)
+        for step in range(M_TILES + 2):
+            if step < M_TILES:
+                add_turned(last, [step], spare=(step % 2 == 1))
+            if 0 <= step - 1 < M_TILES:
+                quantise_z(1, [step - 1])
+            if 0 <= step - 2 < M_TILES:
+                scores(ys[step - 2], 1, step - 2)
+        for mt in all_mts:
+            finish(ys[mt], mt)

@@ -27,6 +27,7 @@ M_TILES = M // P
 N_TILES = N // P
 TILES_PER_PASS = PASS // P
 W1_CHUNKS = [128, 128, 256, 256, 256]
+SHARED_FROM = 4
 
 
 def tile_list_cruise_slot_corrections_kernel(
@@ -40,7 +41,7 @@ def tile_list_cruise_slot_corrections_kernel(
         picks = ctx.enter_context(tc.tile_pool(name="picks", bufs=3))
         tail = ctx.enter_context(tc.tile_pool(name="tail", bufs=4))
         ends = ctx.enter_context(tc.tile_pool(name="ends", bufs=4))
-        sums = ctx.enter_context(tc.psum_pool(name="sums", bufs=5))
+        sums = ctx.enter_context(tc.psum_pool(name="sums", bufs=4))
         turns = ctx.enter_context(tc.psum_pool(name="turns", bufs=2))
 
         offs_sb = keep.tile([P, S // 16], U16, name="offs_sb")
@@ -48,24 +49,15 @@ def tile_list_cruise_slot_corrections_kernel(
 
         tab_sc = keep.tile([P, T], U8, name="tab_sc", tag="tab_sc", align_bytes=64)
         nc.gpsimd.memset(tab_sc[:].bitcast(I32), 0)
-        v_sc1 = keep.tile([P, S], U8, name="v_sc1", align_bytes=64)
         w2_sc = keep.tile([P, 2, H], U8, name="w2_sc", align_bytes=64)
         nc.vector.memset(w2_sc[:].rearrange("p a c -> p (a c)").bitcast(I32), 0)
-        nc.vector.memset(v_sc1[:].bitcast(I32), 0)
-        w4_sc = keep.tile([P, 2, N], U8, name="w4_sc", align_bytes=64)
-        nc.vector.memset(w4_sc[:].rearrange("p a c -> p (a c)").bitcast(I32), 0)
-        ident = keep.tile([P, P], F32, name="ident")
-        make_identity(nc, ident[:])
         for q in range(QUADS):
             nc.gpsimd.dma_start(
                 w2_sc[32 * q : 32 * q + 4, :, :].bitcast(I32),
                 w2_scales[:, 4 * q : 4 * q + 4, :].rearrange("a r c -> r a c").bitcast(I32),
             )
-        for q in range(QUADS):
-            nc.gpsimd.dma_start(
-                w4_sc[32 * q : 32 * q + 4, :, :].bitcast(I32),
-                w4_scales[:, 4 * q : 4 * q + 4, :].rearrange("a r c -> r a c").bitcast(I32),
-            )
+        ident = keep.tile([P, P], F32, name="ident")
+        make_identity(nc, ident[:])
 
         tab_w = [keep.tile([P, T], I32, name=f"tab_w{a}", tag=f"tab_w{a}", align_bytes=64) for a in range(2)]
 
@@ -75,7 +67,10 @@ def tile_list_cruise_slot_corrections_kernel(
         def load_w1(c):
             cols = slice(chunk_start[c], chunk_start[c] + W1_CHUNKS[c])
             for a in range(2):
-                raw = w1_ring.tile([P, PACK, W1_CHUNKS[c]], F32, name="w1_raw", tag="w1_raw", align_bytes=64)
+                if c == 0:
+                    raw = keep.tile([P, PACK, W1_CHUNKS[c]], F32, name="w1_first", tag=f"w1_first{a}", align_bytes=64)
+                else:
+                    raw = w1_ring.tile([P, PACK, W1_CHUNKS[c]], F32, name="w1_raw", tag="w1_raw", align_bytes=64)
                 nc.sync.dma_start(raw[:], w1[a * PASS : (a + 1) * PASS, cols].rearrange("(p j) c -> p j c", j=PACK))
                 w1_raw[c, a] = raw
 
@@ -88,6 +83,7 @@ def tile_list_cruise_slot_corrections_kernel(
         load_w1(0)
         nc.sync.dma_start(tab_w[1][:], tab_words[1].rearrange("p t i -> p (t i)").bitcast(I32))
         load_w1(1)
+        load_w1(2)
         w2_w = keep.tile([P, 2, 2 * H], U8, name="w2_w", align_bytes=64)
         nc.sync.dma_start(w2_w[:].bitcast(I32), w2_words.rearrange("a p c -> p a c").bitcast(I32))
 
@@ -103,6 +99,8 @@ def tile_list_cruise_slot_corrections_kernel(
                 v_w[half, a] = words
 
         nc.vector.tensor_copy(v_sc[:], tab_sc[:].indirect(offs_sb[:]))
+        v_sc1 = keep.tile([P, S], U8, name="v_sc1", tag="w1_first1", align_bytes=64)
+        nc.vector.tensor_copy(v_sc1[:].bitcast(I32), v_sc[:].bitcast(I32))
         for q in range(QUADS):
             nc.scalar.dma_start(v_sc1[32 * q : 32 * q + 4, :].bitcast(I32), v_sc[32 * q + 4 : 32 * q + 8, :].bitcast(I32))
         gather_words(0)
@@ -110,96 +108,89 @@ def tile_list_cruise_slot_corrections_kernel(
 
         w1_codes, w1_sc = {}, {}
 
-        def quantise_w1(c):
-            width = W1_CHUNKS[c]
+        def quantise_w1(rt):
+            c = max(i for i, start in enumerate(chunk_start) if start <= rt * P)
+            cols = slice(rt * P - chunk_start[c], (rt + 1) * P - chunk_start[c])
+            grouped = w1_ring.tile([P, 2, P, PACK], BF16, name="w1_grouped", align_bytes=64)
             for a in range(2):
-                grouped = w1_ring.tile([P, width, PACK], BF16, name="w1_grouped", align_bytes=64)
-                nc.scalar.copy(
-                    grouped[:].rearrange("p (c i) j -> p c j i", i=4),
-                    w1_raw[c, a][:].rearrange("p j (c i) -> p c j i", i=4),
+                copy = nc.vector.tensor_copy if (a == 1 and rt >= SHARED_FROM) else nc.scalar.copy
+                copy(
+                    grouped[:, a].rearrange("p (c i) j -> p c j i", i=4),
+                    w1_raw[c, a][:, :, cols].rearrange("p j (c i) -> p c j i", i=4),
                 )
-                codes = keep.tile([P, width], U32, name=f"w1_codes{c}{a}", align_bytes=64)
-                scales = keep.tile([P, width], U8, name=f"w1_sc{c}{a}", align_bytes=64)
-                nc.vector.quantize_mx(
-                    out=codes[:].bitcast(E4M3), scales=scales[:], in_=grouped[:].rearrange("p c j -> p (c j)")
+            codes = keep.tile([P, 2 * P], U32, name=f"w1_codes{rt}", align_bytes=64)
+            scales = keep.tile([P, 2 * P], U8, name=f"w1_sc{rt}", align_bytes=64)
+            nc.vector.quantize_mx(
+                out=codes[:].bitcast(E4M3), scales=scales[:], in_=grouped[:].rearrange("p a c j -> p (a c j)")
+            )
+            w1_codes[rt], w1_sc[rt] = codes, scales
+
+        win = {}
+        shared = [turns.tile([P, BANK], F32, name=f"shared{i}", bufs=1) for i in range(2)]
+
+        def feature_bank(rt, kind, half):
+            if (rt, kind) not in win:
+                win[rt, kind] = windows.tile([P, S], F32, name=kind)
+            cols = slice(half * BANK, (half + 1) * BANK)
+            acc = sums.tile([P, BANK], F32, name="acc")
+            for a in range(2):
+                if kind == "h":
+                    weights = w1_codes[rt][:, a * P : (a + 1) * P].bitcast(E4M3)
+                    weight_sc = w1_sc[rt][:, a * P : (a + 1) * P]
+                    moving_sc = v_sc[4 * a :, cols]
+                else:
+                    weights = w2_w[:, a, 2 * P * rt : 2 * P * (rt + 1)].bitcast(E2M1)
+                    weight_sc = w2_sc[:, a, P * rt : P * (rt + 1)]
+                    moving_sc = (v_sc, v_sc1)[a][:, cols]
+                nc.tensor.matmul_mx(
+                    out=acc[:],
+                    lhsT=weights,
+                    lhsT_scale=weight_sc,
+                    rhs=v_w[half, a].bitcast(E4M3),
+                    rhs_scale=moving_sc,
+                    start=(a == 0),
+                    stop=(a == 1),
                 )
-                for rt in range(chunk_start[c] // P, (chunk_start[c] + width) // P):
-                    cols = slice(rt * P - chunk_start[c], (rt + 1) * P - chunk_start[c])
-                    w1_codes[rt, a] = codes[:, cols]
-                    w1_sc[rt, a] = scales[:, cols]
+            nc.scalar.copy(win[rt, kind][:, cols], acc[:])
 
-        h_win, e_win = {}, {}
-
-        def features(rt):
-            h = windows.tile([P, S], F32, name="h")
-            e = windows.tile([P, S], F32, name="e")
-            def berth(half, a):
-                return w1_codes[rt, a].bitcast(E4M3), w1_sc[rt, a], v_sc[4 * a :, half * BANK : (half + 1) * BANK]
-
-            def excursion(half, a):
-                return (
-                    w2_w[:, a, 2 * P * rt : 2 * P * (rt + 1)].bitcast(E2M1),
-                    w2_sc[:, a, P * rt : P * (rt + 1)],
-                    (v_sc, v_sc1)[a][:, half * BANK : (half + 1) * BANK],
-                )
-
-            jobs = [(h, berth), (e, excursion)]
-            for window, operands in jobs if rt < R_TILES - 1 else reversed(jobs):
-                for half in range(S // BANK):
-                    acc = sums.tile([P, BANK], F32, name="acc")
-                    for a in range(2):
-                        weights, weight_sc, moving_sc = operands(half, a)
-                        nc.tensor.matmul_mx(
-                            out=acc[:],
-                            lhsT=weights,
-                            lhsT_scale=weight_sc,
-                            rhs=v_w[half, a].bitcast(E4M3),
-                            rhs_scale=moving_sc,
-                            start=(a == 0),
-                            stop=(a == 1),
-                        )
-                    nc.scalar.copy(window[:, half * BANK : (half + 1) * BANK], acc[:])
-            h_win[rt], e_win[rt] = h, e
-
-        dock_abs, prod = {}, {}
+        prod = {}
 
         def places(which, mts):
             return pos_sb[which][:, mts[0] * (P // 16) : (mts[-1] + 1) * (P // 16)]
 
+        das = [keep.tile([P, M], F32, name=f"dock_abs{i}") for i in range(2)]
+
         def pick_dock(rt):
             dock = picks.tile([P, M], F32, name="dock")
-            da = picks.tile([P, M], F32, name="dock_abs")
-            nc.vector.tensor_copy(dock[:], h_win[rt][:].indirect(pos_sb[0][:]))
-            nc.scalar.activation(da[:], dock[:], ACT.Abs)
-            for mt in range(M_TILES):
-                dock_abs[rt, mt] = da[:, mt * P : (mt + 1) * P]
+            nc.vector.tensor_copy(dock[:], win[rt, "h"][:].indirect(pos_sb[0][:]))
+            return dock
+
+        def magnitude(dock, rt):
+            nc.scalar.activation(das[rt % 2][:], dock[:], ACT.Abs)
 
         def pick_sail(rt, mts, pool):
             sail = pool.tile([P, len(mts) * P], F32, name="sail")
-            nc.vector.tensor_copy(sail[:], h_win[rt][:].indirect(places(2, mts)))
+            nc.vector.tensor_copy(sail[:], win[rt, "h"][:].indirect(places(2, mts)))
             return sail
 
         def pick_tour(rt, mts, pool, sail):
             pr = pool.tile([P, len(mts) * P], F32, name="prod")
-            nc.vector.tensor_tensor(pr[:], e_win[rt][:].indirect(places(1, mts)), sail[:], ALU.mult)
+            nc.vector.tensor_tensor(pr[:], win[rt, "e"][:].indirect(places(1, mts)), sail[:], ALU.mult)
             for i, mt in enumerate(mts):
                 prod[rt, mt] = pr[:, i * P : (i + 1) * P]
 
         z_t = [keep.tile([P, M_TILES * PASS], BF16, name=f"z_t{b}", align_bytes=64) for b in range(2)]
 
-        def add_turned(rt, mts, spare=False):
+        def add_turned(rt, mts, bank):
             b, j = divmod(rt, TILES_PER_PASS)
-            if spare:
-                turned = sums.tile([P, len(mts), P], F32, name="acc")
-            else:
-                turned = turns.tile([P, len(mts), P], F32, name="turned", bufs=1)
+            turned = bank[:, : len(mts) * P].rearrange("p (t r) -> p t r", r=P)
             for i, mt in enumerate(mts):
                 nc.tensor.matmul(turned[:, i, :], prod[rt, mt], ident[:], start=True, stop=False, is_transpose=True)
-                nc.tensor.matmul(turned[:, i, :], dock_abs[rt, mt], ident[:], start=False, stop=True, is_transpose=True)
+                nc.tensor.matmul(turned[:, i, :], das[rt % 2][:, mt * P : (mt + 1) * P], ident[:], start=False, stop=True, is_transpose=True)
             dst = z_t[b][:, mts[0] * PASS : (mts[-1] + 1) * PASS].rearrange(
                 "p (t u j q e) -> p t u j q e", u=2, j=TILES_PER_PASS, q=32, e=2
             )[:, :, :, j, :, :]
-            nc.scalar.copy(dst, turned[:].rearrange("p t (q u e) -> p t u q e", u=2, e=2))
+            nc.scalar.copy(dst, turned.rearrange("p t (q u e) -> p t u q e", u=2, e=2))
 
         z_codes = [keep.tile([P, M], U32, name=f"z_codes{b}", align_bytes=64) for b in range(2)]
         z_sc = [keep.tile([P, M], U8, name=f"z_sc{b}", align_bytes=64) for b in range(2)]
@@ -231,64 +222,86 @@ def tile_list_cruise_slot_corrections_kernel(
                 for i in range(2):
                     second[2 * half + i] = part[:, :, i * P : (i + 1) * P]
 
+        def load_w4_scales():
+            spent = w1_codes[2]
+            for q in range(QUADS):
+                nc.sync.dma_start(
+                    spent[32 * q : 32 * q + 4, :].bitcast(I32).rearrange("r (a c) -> r a c", a=2),
+                    w4_scales[:, 4 * q : 4 * q + 4, :].rearrange("a r c -> r a c").bitcast(I32),
+                )
+            second["w4_sc"] = spent[:].bitcast(U8)
+
         def scores(y, b, mt):
             cols = slice(mt * P, (mt + 1) * P)
             for nt in range(N_TILES):
                 nc.tensor.matmul_mx(
                     out=y[:, nt, :],
                     lhsT=second["w4_w"][:, b, nt * P : (nt + 1) * P].bitcast(E4M3),
-                    lhsT_scale=w4_sc[:, b, nt * P : (nt + 1) * P],
+                    lhsT_scale=second["w4_sc"][:, b * N + nt * P : b * N + (nt + 1) * P],
                     rhs=z_codes[b][:, cols].bitcast(E4M3),
                     rhs_scale=z_sc[b][:, cols],
                     start=(b == 0 and nt == 0),
                     stop=(b == 1 and nt == N_TILES - 1),
                 )
 
-        def finish(y, mt):
-            cols = slice(mt * P, (mt + 1) * P)
+        def residual(y, mt):
             res = ends.tile([P, N_TILES, P], F32, name="res")
             sq = ends.tile([P, N_TILES, P], F32, name="sq")
-            cube = ends.tile([P, N_TILES, P], F32, name="cube", bufs=4)
             nc.vector.tensor_tensor(res[:], second[mt], y[:], ALU.subtract)
             nc.scalar.activation(sq[:], res[:], ACT.Square)
+            return res, sq
+
+        def finish(res, sq, mt):
+            cols = slice(mt * P, (mt + 1) * P)
+            cube = ends.tile([P, N_TILES, P], F32, name="cube")
             nc.vector.tensor_tensor(cube[:], sq[:], res[:], ALU.mult)
             nc.sync.dma_start(out.rearrange("(t p) m -> p t m", p=P)[:, :, cols], cube[:])
 
         all_mts = list(range(M_TILES))
         last = R_TILES - 1
-        chunk_of = {chunk_start[c] // P: c for c in range(len(W1_CHUNKS))}
 
-        def prepare(rt):
-            if rt in chunk_of:
-                c = chunk_of[rt]
-                quantise_w1(c)
-                if c + 2 < len(W1_CHUNKS):
-                    load_w1(c + 2)
-                if c + 2 == len(W1_CHUNKS) - 1:
-                    load_second_stage()
+        def banks(rt):
+            kinds = ("h", "e") if rt < last else ("e", "h")
+            return [(rt, kind, half) for kind in kinds for half in range(2)]
 
-        prepare(0)
-        prepare(1)
-        features(0)
-        prepare(2)
-        features(1)
-        prepare(4)
+        quantise_w1(0)
+        quantise_w1(1)
+        load_w1(3)
+        for job in banks(0):
+            feature_bank(*job)
+        quantise_w1(2)
+        for job in banks(1)[:2]:
+            feature_bank(*job)
+        quantise_w1(3)
+        load_w1(4)
+        for job in banks(1)[2:]:
+            feature_bank(*job)
         for rt in range(last):
+            dock = pick_dock(rt)
             sail = pick_sail(rt, all_mts, picks)
-            pick_dock(rt)
             pick_tour(rt, all_mts, picks, sail)
+            between = [lambda: magnitude(dock, rt)]
             if rt >= 1:
-                add_turned(rt - 1, all_mts)
+                between.insert(0, lambda: add_turned(rt - 1, all_mts, shared[0]))
+            if rt + 4 < R_TILES:
+                between.append(lambda: quantise_w1(rt + 4))
             if rt == TILES_PER_PASS:
-                quantise_z(0, [0, 1])
-                quantise_z(0, [2, 3])
-            if rt + 2 < R_TILES:
-                features(rt + 2)
+                between.append(lambda: quantise_z(0, [0, 1]))
+                between.append(lambda: quantise_z(0, [2, 3]))
+            jobs = banks(rt + 2) if rt + 2 < R_TILES else []
+            for i in range(max(len(jobs), len(between))):
+                if i < len(jobs):
+                    feature_bank(*jobs[i])
+                if i < len(between):
+                    between[i]()
             if rt == 1:
-                prepare(6)
-        add_turned(last - 1, all_mts)
+                load_second_stage()
+                load_w4_scales()
         ys = [sums.tile([P, N_TILES, P], F32, name="acc") for mt in all_mts]
-        pick_dock(last)
+        dock = pick_dock(last)
+        add_turned(last - 1, [0, 1], shared[1])
+        add_turned(last - 1, [2, 3], shared[0])
+        magnitude(dock, last)
         sails = [pick_sail(last, [0], tail)]
         for mt in all_mts:
             if mt + 1 < M_TILES:
@@ -298,10 +311,11 @@ def tile_list_cruise_slot_corrections_kernel(
             scores(ys[mt], 0, mt)
         for step in range(M_TILES + 2):
             if step < M_TILES:
-                add_turned(last, [step], spare=(step % 2 == 1))
+                add_turned(last, [step], shared[(step + 1) % 2])
             if 0 <= step - 1 < M_TILES:
                 quantise_z(1, [step - 1])
             if 0 <= step - 2 < M_TILES:
                 scores(ys[step - 2], 1, step - 2)
+        residuals = [residual(ys[mt], mt) for mt in all_mts]
         for mt in all_mts:
-            finish(ys[mt], mt)
+            finish(*residuals[mt], mt)

@@ -20,14 +20,18 @@ ALU = mybir.AluOpType
 P = 128
 PACK = 4
 PASS = P * PACK
+PASSES = 2
 BANK = 512
+HALVES = S // BANK
 QUADS = 4
+LIST_COL = 16
 R_TILES = H // P
 M_TILES = M // P
 N_TILES = N // P
 TILES_PER_PASS = PASS // P
 W1_CHUNKS = [128, 128, 256, 256, 256]
-SHARED_FROM = 4
+FEATURES_AHEAD = 2
+W1_AHEAD = 4
 
 
 def tile_list_cruise_slot_corrections_kernel(
@@ -37,19 +41,20 @@ def tile_list_cruise_slot_corrections_kernel(
     with ExitStack() as ctx:
         keep = ctx.enter_context(tc.tile_pool(name="keep", bufs=1))
         w1_ring = ctx.enter_context(tc.tile_pool(name="w1_ring", bufs=4))
-        windows = ctx.enter_context(tc.tile_pool(name="windows", bufs=3))
+        windows = ctx.enter_context(tc.tile_pool(name="windows", bufs=FEATURES_AHEAD + 1))
         picks = ctx.enter_context(tc.tile_pool(name="picks", bufs=3))
-        tail = ctx.enter_context(tc.tile_pool(name="tail", bufs=4))
-        ends = ctx.enter_context(tc.tile_pool(name="ends", bufs=4))
+        tail = ctx.enter_context(tc.tile_pool(name="tail", bufs=M_TILES))
+        ends = ctx.enter_context(tc.tile_pool(name="ends", bufs=M_TILES))
         sums = ctx.enter_context(tc.psum_pool(name="sums", bufs=4))
         turns = ctx.enter_context(tc.psum_pool(name="turns", bufs=2))
 
-        offs_sb = keep.tile([P, S // 16], U16, name="offs_sb")
-        pos_sb = [keep.tile([P, M // 16], U16, name=f"pos{i + 1}_sb") for i in range(3)]
+        offs_sb = keep.tile([P, S // LIST_COL], U16, name="offs_sb")
+        pos_sb = [keep.tile([P, M // LIST_COL], U16, name=f"pos{i + 1}_sb") for i in range(3)]
+        DOCK, TOUR, SAIL = 0, 1, 2
 
         tab_sc = keep.tile([P, T], U8, name="tab_sc", tag="tab_sc", align_bytes=64)
         nc.gpsimd.memset(tab_sc[:].bitcast(I32), 0)
-        w2_sc = keep.tile([P, 2, H], U8, name="w2_sc", align_bytes=64)
+        w2_sc = keep.tile([P, PASSES, H], U8, name="w2_sc", align_bytes=64)
         nc.vector.memset(w2_sc[:].rearrange("p a c -> p (a c)").bitcast(I32), 0)
         for q in range(QUADS):
             nc.gpsimd.dma_start(
@@ -59,14 +64,14 @@ def tile_list_cruise_slot_corrections_kernel(
         ident = keep.tile([P, P], F32, name="ident")
         make_identity(nc, ident[:])
 
-        tab_w = [keep.tile([P, T], I32, name=f"tab_w{a}", tag=f"tab_w{a}", align_bytes=64) for a in range(2)]
+        tab_w = [keep.tile([P, T], I32, name=f"tab_w{a}", tag=f"tab_w{a}", align_bytes=64) for a in range(PASSES)]
 
         chunk_start = [sum(W1_CHUNKS[:c]) for c in range(len(W1_CHUNKS))]
         w1_raw = {}
 
         def load_w1(c):
             cols = slice(chunk_start[c], chunk_start[c] + W1_CHUNKS[c])
-            for a in range(2):
+            for a in range(PASSES):
                 if c == 0:
                     raw = keep.tile([P, PACK, W1_CHUNKS[c]], F32, name="w1_first", tag=f"w1_first{a}", align_bytes=64)
                 else:
@@ -74,66 +79,72 @@ def tile_list_cruise_slot_corrections_kernel(
                 nc.sync.dma_start(raw[:], w1[a * PASS : (a + 1) * PASS, cols].rearrange("(p j) c -> p j c", j=PACK))
                 w1_raw[c, a] = raw
 
+        def load_table_words(a):
+            nc.sync.dma_start(tab_w[a][:], tab_words[a].rearrange("p t i -> p (t i)").bitcast(I32))
+
         nc.sync.dma_start(offs_sb[:], offs)
         for sb, pos in zip(pos_sb, (pos1, pos2, pos3)):
             nc.sync.dma_start(sb[:], pos)
-        nc.sync.dma_start(tab_w[0][:], tab_words[0].rearrange("p t i -> p (t i)").bitcast(I32))
         for q in range(QUADS):
-            nc.scalar.dma_start(tab_sc[32 * q : 32 * q + 8, :].bitcast(I32), tab_scales[:, 4 * q : 4 * q + 4, :].bitcast(I32))
+            nc.sync.dma_start(
+                tab_sc[32 * q : 32 * q + 8, :].bitcast(I32), tab_scales[:, 4 * q : 4 * q + 4, :].bitcast(I32)
+            )
+        load_table_words(0)
         load_w1(0)
-        nc.sync.dma_start(tab_w[1][:], tab_words[1].rearrange("p t i -> p (t i)").bitcast(I32))
+        load_table_words(1)
         load_w1(1)
         load_w1(2)
-        w2_w = keep.tile([P, 2, 2 * H], U8, name="w2_w", align_bytes=64)
+        w2_w = keep.tile([P, PASSES, 2 * H], U8, name="w2_w", align_bytes=64)
         nc.sync.dma_start(w2_w[:].bitcast(I32), w2_words.rearrange("a p c -> p a c").bitcast(I32))
 
         v_sc = keep.tile([P, S], U8, name="v_sc", align_bytes=64)
-        v_words = keep.tile([P, 2 * S], U32, name="v_words", tag="tab_sc", align_bytes=64)
+        v_words = keep.tile([P, PASSES * S], U32, name="v_words", tag="tab_sc", align_bytes=64)
         v_w = {}
 
-        def gather_words(a):
-            for half in range(S // BANK):
-                lst = offs_sb[:, half * (BANK // 16) : (half + 1) * (BANK // 16)]
-                words = v_words[:, a * S + half * BANK : a * S + (half + 1) * BANK]
-                nc.vector.tensor_copy(words, tab_w[a][:].bitcast(U32).indirect(lst))
-                v_w[half, a] = words
+        def gather_words(a, half):
+            entries = offs_sb[:, half * (BANK // LIST_COL) : (half + 1) * (BANK // LIST_COL)]
+            words = v_words[:, a * S + half * BANK : a * S + (half + 1) * BANK]
+            nc.vector.tensor_copy(words, tab_w[a][:].bitcast(U32).indirect(entries))
+            v_w[half, a] = words
 
         nc.vector.tensor_copy(v_sc[:], tab_sc[:].indirect(offs_sb[:]))
+        gather_words(0, 0)
         v_sc1 = keep.tile([P, S], U8, name="v_sc1", tag="w1_first1", align_bytes=64)
         nc.vector.tensor_copy(v_sc1[:].bitcast(I32), v_sc[:].bitcast(I32))
         for q in range(QUADS):
-            nc.scalar.dma_start(v_sc1[32 * q : 32 * q + 4, :].bitcast(I32), v_sc[32 * q + 4 : 32 * q + 8, :].bitcast(I32))
-        gather_words(0)
-        gather_words(1)
+            nc.scalar.dma_start(
+                v_sc1[32 * q : 32 * q + 4, :].bitcast(I32), v_sc[32 * q + 4 : 32 * q + 8, :].bitcast(I32)
+            )
+        gather_words(0, 1)
+        for half in range(HALVES):
+            gather_words(1, half)
 
         w1_codes, w1_sc = {}, {}
 
         def quantise_w1(rt):
             c = max(i for i, start in enumerate(chunk_start) if start <= rt * P)
             cols = slice(rt * P - chunk_start[c], (rt + 1) * P - chunk_start[c])
-            grouped = w1_ring.tile([P, 2, P, PACK], BF16, name="w1_grouped", align_bytes=64)
-            for a in range(2):
-                copy = nc.vector.tensor_copy if (a == 1 and rt >= SHARED_FROM) else nc.scalar.copy
-                copy(
+            grouped = w1_ring.tile([P, PASSES, P, PACK], BF16, name="w1_grouped", align_bytes=64)
+            for a in range(PASSES):
+                nc.scalar.copy(
                     grouped[:, a].rearrange("p (c i) j -> p c j i", i=4),
                     w1_raw[c, a][:, :, cols].rearrange("p j (c i) -> p c j i", i=4),
                 )
-            codes = keep.tile([P, 2 * P], U32, name=f"w1_codes{rt}", align_bytes=64)
-            scales = keep.tile([P, 2 * P], U8, name=f"w1_sc{rt}", align_bytes=64)
+            codes = keep.tile([P, PASSES * P], U32, name=f"w1_codes{rt}", align_bytes=64)
+            scales = keep.tile([P, PASSES * P], U8, name=f"w1_sc{rt}", align_bytes=64)
             nc.vector.quantize_mx(
                 out=codes[:].bitcast(E4M3), scales=scales[:], in_=grouped[:].rearrange("p a c j -> p (a c j)")
             )
             w1_codes[rt], w1_sc[rt] = codes, scales
 
         win = {}
-        shared = [turns.tile([P, BANK], F32, name=f"shared{i}", bufs=1) for i in range(2)]
 
         def feature_bank(rt, kind, half):
             if (rt, kind) not in win:
                 win[rt, kind] = windows.tile([P, S], F32, name=kind)
             cols = slice(half * BANK, (half + 1) * BANK)
             acc = sums.tile([P, BANK], F32, name="acc")
-            for a in range(2):
+            for a in range(PASSES):
                 if kind == "h":
                     weights = w1_codes[rt][:, a * P : (a + 1) * P].bitcast(E4M3)
                     weight_sc = w1_sc[rt][:, a * P : (a + 1) * P]
@@ -149,51 +160,57 @@ def tile_list_cruise_slot_corrections_kernel(
                     rhs=v_w[half, a].bitcast(E4M3),
                     rhs_scale=moving_sc,
                     start=(a == 0),
-                    stop=(a == 1),
+                    stop=(a == PASSES - 1),
                 )
             nc.scalar.copy(win[rt, kind][:, cols], acc[:])
 
+        last = R_TILES - 1
         prod = {}
 
         def places(which, mts):
-            return pos_sb[which][:, mts[0] * (P // 16) : (mts[-1] + 1) * (P // 16)]
+            return pos_sb[which][:, mts[0] * (P // LIST_COL) : (mts[-1] + 1) * (P // LIST_COL)]
 
-        das = [keep.tile([P, M], F32, name=f"dock_abs{i}") for i in range(2)]
+        dock_abs_tiles = [keep.tile([P, M], F32, name=f"dock_abs{i}") for i in range(2)]
+
+        def dock_abs(rt):
+            return dock_abs_tiles[min(rt, last - 1) % 2]
 
         def pick_dock(rt):
             dock = picks.tile([P, M], F32, name="dock")
-            nc.vector.tensor_copy(dock[:], win[rt, "h"][:].indirect(pos_sb[0][:]))
+            nc.vector.tensor_copy(dock[:], win[rt, "h"][:].indirect(pos_sb[DOCK][:]))
             return dock
 
         def magnitude(dock, rt):
-            nc.scalar.activation(das[rt % 2][:], dock[:], ACT.Abs)
+            nc.scalar.activation(dock_abs(rt)[:], dock[:], ACT.Abs)
 
         def pick_sail(rt, mts, pool):
             sail = pool.tile([P, len(mts) * P], F32, name="sail")
-            nc.vector.tensor_copy(sail[:], win[rt, "h"][:].indirect(places(2, mts)))
+            nc.vector.tensor_copy(sail[:], win[rt, "h"][:].indirect(places(SAIL, mts)))
             return sail
 
-        def pick_tour(rt, mts, pool, sail):
-            pr = pool.tile([P, len(mts) * P], F32, name="prod")
-            nc.vector.tensor_tensor(pr[:], win[rt, "e"][:].indirect(places(1, mts)), sail[:], ALU.mult)
+        def pick_tour_times(sail, rt, mts, pool):
+            product = pool.tile([P, len(mts) * P], F32, name="prod")
+            nc.vector.tensor_tensor(product[:], win[rt, "e"][:].indirect(places(TOUR, mts)), sail[:], ALU.mult)
             for i, mt in enumerate(mts):
-                prod[rt, mt] = pr[:, i * P : (i + 1) * P]
+                prod[rt, mt] = product[:, i * P : (i + 1) * P]
 
-        z_t = [keep.tile([P, M_TILES * PASS], BF16, name=f"z_t{b}", align_bytes=64) for b in range(2)]
+        z_t = [keep.tile([P, M_TILES * PASS], BF16, name=f"z_t{b}", align_bytes=64) for b in range(PASSES)]
+        add_banks = [turns.tile([P, BANK], F32, name=f"add_bank{i}", bufs=1) for i in range(2)]
 
         def add_turned(rt, mts, bank):
             b, j = divmod(rt, TILES_PER_PASS)
             turned = bank[:, : len(mts) * P].rearrange("p (t r) -> p t r", r=P)
             for i, mt in enumerate(mts):
-                nc.tensor.matmul(turned[:, i, :], prod[rt, mt], ident[:], start=True, stop=False, is_transpose=True)
-                nc.tensor.matmul(turned[:, i, :], das[rt % 2][:, mt * P : (mt + 1) * P], ident[:], start=False, stop=True, is_transpose=True)
+                magnitudes = dock_abs(rt)[:, mt * P : (mt + 1) * P]
+                nc.tensor.matmul(turned[:, i, :], magnitudes, ident[:], start=True, stop=False, is_transpose=True)
+                nc.tensor.matmul(turned[:, i, :], prod[rt, mt], ident[:], start=False, stop=True, is_transpose=True)
             dst = z_t[b][:, mts[0] * PASS : (mts[-1] + 1) * PASS].rearrange(
                 "p (t u j q e) -> p t u j q e", u=2, j=TILES_PER_PASS, q=32, e=2
             )[:, :, :, j, :, :]
             nc.scalar.copy(dst, turned.rearrange("p t (q u e) -> p t u q e", u=2, e=2))
 
-        z_codes = [keep.tile([P, M], U32, name=f"z_codes{b}", align_bytes=64) for b in range(2)]
-        z_sc = [keep.tile([P, M], U8, name=f"z_sc{b}", align_bytes=64) for b in range(2)]
+        z_codes = [keep.tile([P, M], U32, name=f"z_codes{b}", align_bytes=64) for b in range(PASSES)]
+        z_sc = [keep.tile([P, M], U8, name=f"z_sc{b}", align_bytes=64) for b in range(PASSES)]
 
         def quantise_z(b, mts):
             back = turns.tile([P, len(mts), 2, P], F32, name="back")
@@ -209,45 +226,40 @@ def tile_list_cruise_slot_corrections_kernel(
             cols = slice(mts[0] * P, (mts[-1] + 1) * P)
             nc.vector.quantize_mx(out=z_codes[b][:, cols].bitcast(E4M3), scales=z_sc[b][:, cols], in_=grouped[:])
 
-        second = {}
-
         def load_second_stage():
-            w4_w = w1_ring.tile([P, 2, N], I32, name="w4_w", tag="w1_raw", align_bytes=64)
-            second["w4_w"] = w4_w
+            w4_w = w1_ring.tile([P, PASSES, N], I32, name="w4_w", tag="w1_raw", align_bytes=64)
             nc.sync.dma_start(w4_w[:], w4_words.rearrange("a p c i -> p a (c i)").bitcast(I32))
+            targets = []
             for half in range(2):
                 part = w1_ring.tile([P, N_TILES, M // 2], F32, name="target_sb", tag="w1_raw", align_bytes=64)
                 cols = slice(half * (M // 2), (half + 1) * (M // 2))
                 nc.sync.dma_start(part[:], target.rearrange("(t p) m -> p t m", p=P)[:, :, cols])
-                for i in range(2):
-                    second[2 * half + i] = part[:, :, i * P : (i + 1) * P]
-
-        def load_w4_scales():
+                targets.extend(part[:, :, i * P : (i + 1) * P] for i in range(M_TILES // 2))
             spent = w1_codes[2]
             for q in range(QUADS):
                 nc.sync.dma_start(
-                    spent[32 * q : 32 * q + 4, :].bitcast(I32).rearrange("r (a c) -> r a c", a=2),
+                    spent[32 * q : 32 * q + 4, :].bitcast(I32).rearrange("r (a c) -> r a c", a=PASSES),
                     w4_scales[:, 4 * q : 4 * q + 4, :].rearrange("a r c -> r a c").bitcast(I32),
                 )
-            second["w4_sc"] = spent[:].bitcast(U8)
+            return w4_w, spent[:].bitcast(U8), targets
 
         def scores(y, b, mt):
             cols = slice(mt * P, (mt + 1) * P)
             for nt in range(N_TILES):
                 nc.tensor.matmul_mx(
                     out=y[:, nt, :],
-                    lhsT=second["w4_w"][:, b, nt * P : (nt + 1) * P].bitcast(E4M3),
-                    lhsT_scale=second["w4_sc"][:, b * N + nt * P : b * N + (nt + 1) * P],
+                    lhsT=w4_w[:, b, nt * P : (nt + 1) * P].bitcast(E4M3),
+                    lhsT_scale=w4_sc[:, b * N + nt * P : b * N + (nt + 1) * P],
                     rhs=z_codes[b][:, cols].bitcast(E4M3),
                     rhs_scale=z_sc[b][:, cols],
                     start=(b == 0 and nt == 0),
-                    stop=(b == 1 and nt == N_TILES - 1),
+                    stop=(b == PASSES - 1 and nt == N_TILES - 1),
                 )
 
         def residual(y, mt):
             res = ends.tile([P, N_TILES, P], F32, name="res")
             sq = ends.tile([P, N_TILES, P], F32, name="sq")
-            nc.vector.tensor_tensor(res[:], second[mt], y[:], ALU.subtract)
+            nc.vector.tensor_tensor(res[:], targets[mt], y[:], ALU.subtract)
             nc.scalar.activation(sq[:], res[:], ACT.Square)
             return res, sq
 
@@ -258,11 +270,10 @@ def tile_list_cruise_slot_corrections_kernel(
             nc.sync.dma_start(out.rearrange("(t p) m -> p t m", p=P)[:, :, cols], cube[:])
 
         all_mts = list(range(M_TILES))
-        last = R_TILES - 1
 
         def banks(rt):
             kinds = ("h", "e") if rt < last else ("e", "h")
-            return [(rt, kind, half) for kind in kinds for half in range(2)]
+            return [(rt, kind, half) for kind in kinds for half in range(HALVES)]
 
         quantise_w1(0)
         quantise_w1(1)
@@ -270,48 +281,50 @@ def tile_list_cruise_slot_corrections_kernel(
         for job in banks(0):
             feature_bank(*job)
         quantise_w1(2)
-        for job in banks(1)[:2]:
+        for job in banks(1)[:HALVES]:
             feature_bank(*job)
         quantise_w1(3)
         load_w1(4)
-        for job in banks(1)[2:]:
+        for job in banks(1)[HALVES:]:
             feature_bank(*job)
+
         for rt in range(last):
-            dock = pick_dock(rt)
             sail = pick_sail(rt, all_mts, picks)
-            pick_tour(rt, all_mts, picks, sail)
-            between = [lambda: magnitude(dock, rt)]
+            dock = pick_dock(rt)
+            pick_tour_times(sail, rt, all_mts, picks)
+            between = []
             if rt >= 1:
-                between.insert(0, lambda: add_turned(rt - 1, all_mts, shared[0]))
-            if rt + 4 < R_TILES:
-                between.append(lambda: quantise_w1(rt + 4))
+                between.append(lambda: add_turned(rt - 1, all_mts, add_banks[0]))
+            between.append(lambda: magnitude(dock, rt))
+            if rt + W1_AHEAD < R_TILES:
+                between.append(lambda: quantise_w1(rt + W1_AHEAD))
             if rt == TILES_PER_PASS:
-                between.append(lambda: quantise_z(0, [0, 1]))
-                between.append(lambda: quantise_z(0, [2, 3]))
-            jobs = banks(rt + 2) if rt + 2 < R_TILES else []
+                between.append(lambda: quantise_z(0, all_mts[:2]))
+                between.append(lambda: quantise_z(0, all_mts[2:]))
+            jobs = banks(rt + FEATURES_AHEAD) if rt + FEATURES_AHEAD < R_TILES else []
             for i in range(max(len(jobs), len(between))):
                 if i < len(jobs):
                     feature_bank(*jobs[i])
                 if i < len(between):
                     between[i]()
             if rt == 1:
-                load_second_stage()
-                load_w4_scales()
+                w4_w, w4_sc, targets = load_second_stage()
+
         ys = [sums.tile([P, N_TILES, P], F32, name="acc") for mt in all_mts]
         dock = pick_dock(last)
-        add_turned(last - 1, [0, 1], shared[1])
-        add_turned(last - 1, [2, 3], shared[0])
+        add_turned(last - 1, all_mts[:2], add_banks[1])
+        add_turned(last - 1, all_mts[2:], add_banks[0])
         magnitude(dock, last)
         sails = [pick_sail(last, [0], tail)]
         for mt in all_mts:
             if mt + 1 < M_TILES:
                 sails.append(pick_sail(last, [mt + 1], tail))
-            pick_tour(last, [mt], tail, sails[mt])
+            pick_tour_times(sails[mt], last, [mt], tail)
         for mt in all_mts:
             scores(ys[mt], 0, mt)
         for step in range(M_TILES + 2):
             if step < M_TILES:
-                add_turned(last, [step], shared[(step + 1) % 2])
+                add_turned(last, [step], add_banks[(step + 1) % 2])
             if 0 <= step - 1 < M_TILES:
                 quantise_z(1, [step - 1])
             if 0 <= step - 2 < M_TILES:

@@ -25,13 +25,10 @@ BANK = 512
 HALVES = S // BANK
 QUADS = 4
 LIST_COL = 16
-R_TILES = H // P
-M_TILES = M // P
 N_TILES = N // P
-TILES_PER_PASS = PASS // P
-W1_CHUNKS = [128, 128, 256, 256, 256]
-FEATURES_AHEAD = 2
-W1_AHEAD = 4
+M_TILES = M // P
+PIECES = [(0, 256), (256, 384), (384, 512)]
+TOURS_ON_SCALAR = 0
 
 
 def tile_list_cruise_slot_corrections_kernel(
@@ -40,295 +37,285 @@ def tile_list_cruise_slot_corrections_kernel(
     nc = tc.nc
     with ExitStack() as ctx:
         keep = ctx.enter_context(tc.tile_pool(name="keep", bufs=1))
-        w1_ring = ctx.enter_context(tc.tile_pool(name="w1_ring", bufs=4))
-        windows = ctx.enter_context(tc.tile_pool(name="windows", bufs=FEATURES_AHEAD + 1))
-        picks = ctx.enter_context(tc.tile_pool(name="picks", bufs=3))
-        tail = ctx.enter_context(tc.tile_pool(name="tail", bufs=M_TILES))
-        ends = ctx.enter_context(tc.tile_pool(name="ends", bufs=M_TILES))
-        sums = ctx.enter_context(tc.psum_pool(name="sums", bufs=4))
-        turns = ctx.enter_context(tc.psum_pool(name="turns", bufs=2))
+        ring = ctx.enter_context(tc.tile_pool(name="ring", bufs=2))
+        e_windows = ctx.enter_context(tc.tile_pool(name="e_windows", bufs=8))
+        sums = ctx.enter_context(tc.psum_pool(name="sums", bufs=8))
+
+        def big(shape, dtype, name, buffer):
+            return keep.tile(shape, dtype, name=name, tag=f"big{buffer}", align_bytes=64)
 
         offs_sb = keep.tile([P, S // LIST_COL], U16, name="offs_sb")
         pos_sb = [keep.tile([P, M // LIST_COL], U16, name=f"pos{i + 1}_sb") for i in range(3)]
         DOCK, TOUR, SAIL = 0, 1, 2
 
-        tab_sc = keep.tile([P, T], U8, name="tab_sc", tag="tab_sc", align_bytes=64)
+        tab_sc = big([P, T], U8, "tab_sc", 2)
         nc.gpsimd.memset(tab_sc[:].bitcast(I32), 0)
-        w2_sc = keep.tile([P, PASSES, H], U8, name="w2_sc", align_bytes=64)
-        nc.vector.memset(w2_sc[:].rearrange("p a c -> p (a c)").bitcast(I32), 0)
+        w2_sc_raw = keep.tile([P, PASSES * H], U8, name="w2_sc_raw", align_bytes=64)
+        nc.vector.memset(w2_sc_raw[:].bitcast(I32), 0)
+        v_sc1 = keep.tile([P, S], U8, name="v_sc1", align_bytes=64)
+        nc.vector.memset(v_sc1[:].bitcast(I32), 0)
         for q in range(QUADS):
             nc.gpsimd.dma_start(
-                w2_sc[32 * q : 32 * q + 4, :, :].bitcast(I32),
+                w2_sc_raw[32 * q : 32 * q + 4, :].bitcast(I32).rearrange("r (a c) -> r a c", a=PASSES),
                 w2_scales[:, 4 * q : 4 * q + 4, :].rearrange("a r c -> r a c").bitcast(I32),
             )
+
+        tab_w = [big([P, T], I32, f"tab_w{a}", a) for a in range(PASSES)]
         ident = keep.tile([P, P], F32, name="ident")
         make_identity(nc, ident[:])
-
-        tab_w = [keep.tile([P, T], I32, name=f"tab_w{a}", tag=f"tab_w{a}", align_bytes=64) for a in range(PASSES)]
-
-        chunk_start = [sum(W1_CHUNKS[:c]) for c in range(len(W1_CHUNKS))]
+        w2_raw = keep.tile([P, PASSES, 2 * H], U8, name="w2_raw", align_bytes=64)
         w1_raw = {}
-
-        def load_w1(c):
-            cols = slice(chunk_start[c], chunk_start[c] + W1_CHUNKS[c])
-            for a in range(PASSES):
-                if c == 0:
-                    raw = keep.tile([P, PACK, W1_CHUNKS[c]], F32, name="w1_first", tag=f"w1_first{a}", align_bytes=64)
-                else:
-                    raw = w1_ring.tile([P, PACK, W1_CHUNKS[c]], F32, name="w1_raw", tag="w1_raw", align_bytes=64)
-                nc.sync.dma_start(raw[:], w1[a * PASS : (a + 1) * PASS, cols].rearrange("(p j) c -> p j c", j=PACK))
-                w1_raw[c, a] = raw
 
         def load_table_words(a):
             nc.sync.dma_start(tab_w[a][:], tab_words[a].rearrange("p t i -> p (t i)").bitcast(I32))
 
+        def load_w1(b, a, raw):
+            rows = w1[a * PASS : (a + 1) * PASS, b * PASS : (b + 1) * PASS]
+            nc.sync.dma_start(raw, rows.rearrange("(p j) c -> p j c", j=PACK))
+            w1_raw[b, a] = raw
+
         nc.sync.dma_start(offs_sb[:], offs)
-        for sb, pos in zip(pos_sb, (pos1, pos2, pos3)):
-            nc.sync.dma_start(sb[:], pos)
+        nc.sync.dma_start(pos_sb[TOUR][:], pos2)
+        nc.sync.dma_start(pos_sb[SAIL][:], pos3)
         for q in range(QUADS):
             nc.sync.dma_start(
                 tab_sc[32 * q : 32 * q + 8, :].bitcast(I32), tab_scales[:, 4 * q : 4 * q + 4, :].bitcast(I32)
             )
         load_table_words(0)
-        load_w1(0)
         load_table_words(1)
-        load_w1(1)
-        load_w1(2)
-        w2_w = keep.tile([P, PASSES, 2 * H], U8, name="w2_w", align_bytes=64)
-        nc.sync.dma_start(w2_w[:].bitcast(I32), w2_words.rearrange("a p c -> p a c").bitcast(I32))
+        nc.sync.dma_start(w2_raw[:].bitcast(I32), w2_words.rearrange("a p c -> p a c").bitcast(I32))
+        nc.sync.dma_start(pos_sb[DOCK][:], pos1)
 
         v_sc = keep.tile([P, S], U8, name="v_sc", align_bytes=64)
-        v_words = keep.tile([P, PASSES * S], U32, name="v_words", tag="tab_sc", align_bytes=64)
-        v_w = {}
-
-        def gather_words(a, half):
-            entries = offs_sb[:, half * (BANK // LIST_COL) : (half + 1) * (BANK // LIST_COL)]
-            words = v_words[:, a * S + half * BANK : a * S + (half + 1) * BANK]
-            nc.vector.tensor_copy(words, tab_w[a][:].bitcast(U32).indirect(entries))
-            v_w[half, a] = words
-
         nc.vector.tensor_copy(v_sc[:], tab_sc[:].indirect(offs_sb[:]))
-        gather_words(0, 0)
-        v_sc1 = keep.tile([P, S], U8, name="v_sc1", tag="w1_first1", align_bytes=64)
-        nc.vector.tensor_copy(v_sc1[:].bitcast(I32), v_sc[:].bitcast(I32))
         for q in range(QUADS):
             nc.scalar.dma_start(
                 v_sc1[32 * q : 32 * q + 4, :].bitcast(I32), v_sc[32 * q + 4 : 32 * q + 8, :].bitcast(I32)
             )
-        gather_words(0, 1)
-        for half in range(HALVES):
-            gather_words(1, half)
+        load_w1(0, 0, big([P, PACK, PASS], F32, "w1_raw00", 2)[:])
+        v_w = {}
+
+        def gather_words(a):
+            for half in range(HALVES):
+                entries = offs_sb[:, half * (BANK // LIST_COL) : (half + 1) * (BANK // LIST_COL)]
+                words = keep.tile([P, BANK], U32, name=f"v_w{a}{half}", align_bytes=64)
+                nc.vector.tensor_copy(words[:], tab_w[a][:].bitcast(U32).indirect(entries))
+                v_w[a, half] = words
+
+        gather_words(0)
+        load_w1(0, 1, big([P, PACK, PASS], F32, "w1_raw01", 0)[:])
+        gather_words(1)
+
+        dealt = big([P, 3 * H], U8, "w2_dealt", 1)
+        nc.vector.tensor_copy(
+            dealt[:, : 2 * H].bitcast(U16).rearrange("p (a t q) -> p a q t", a=PASSES, t=PACK),
+            w2_raw[:, :, H:].bitcast(U16).rearrange("p a (q t) -> p a q t", t=PACK),
+        )
+        w2_sc_by_pass = w2_sc_raw[:].rearrange("p (a c) -> p a c", a=PASSES)
+        nc.vector.tensor_copy(
+            dealt[:, 2 * H :].rearrange("p (a t q) -> p a q t", a=PASSES, t=PACK),
+            w2_sc_by_pass[:, :, PASS:].rearrange("p a (q t) -> p a q t", t=PACK),
+        )
+        w2_w = [w2_raw, dealt[:, : 2 * H].rearrange("p (a c) -> p a c", a=PASSES)]
+        w2_sc = [w2_sc_by_pass, dealt[:, 2 * H :].rearrange("p (a c) -> p a c", a=PASSES)]
 
         w1_codes, w1_sc = {}, {}
 
-        def quantise_w1(rt):
-            c = max(i for i, start in enumerate(chunk_start) if start <= rt * P)
-            cols = slice(rt * P - chunk_start[c], (rt + 1) * P - chunk_start[c])
-            grouped = w1_ring.tile([P, PASSES, P, PACK], BF16, name="w1_grouped", align_bytes=64)
-            for a in range(PASSES):
-                nc.scalar.copy(
-                    grouped[:, a].rearrange("p (c i) j -> p c j i", i=4),
-                    w1_raw[c, a][:, :, cols].rearrange("p j (c i) -> p c j i", i=4),
+        def quantise_w1(b, a):
+            grouped = ring.tile([P, PASS, PACK], BF16, name="w1_grouped", align_bytes=64)
+            raw = w1_raw[b, a]
+            if b == 0:
+                nc.vector.tensor_copy(
+                    grouped[:].rearrange("p (c i) j -> p c j i", i=4), raw.rearrange("p j (c i) -> p c j i", i=4)
                 )
-            codes = keep.tile([P, PASSES * P], U32, name=f"w1_codes{rt}", align_bytes=64)
-            scales = keep.tile([P, PASSES * P], U8, name=f"w1_sc{rt}", align_bytes=64)
+            else:
+                nc.vector.tensor_copy(
+                    grouped[:].rearrange("p (t q) j -> p q j t", t=PACK), raw.rearrange("p j (q t) -> p q j t", t=PACK)
+                )
+            codes = keep.tile([P, PASS], U32, name=f"w1_codes{b}{a}", align_bytes=64)
+            scales = keep.tile([P, PASS], U8, name=f"w1_sc{b}{a}", align_bytes=64)
             nc.vector.quantize_mx(
-                out=codes[:].bitcast(E4M3), scales=scales[:], in_=grouped[:].rearrange("p a c j -> p (a c j)")
+                out=codes[:].bitcast(E4M3), scales=scales[:], in_=grouped[:].rearrange("p c j -> p (c j)")
             )
-            w1_codes[rt], w1_sc[rt] = codes, scales
+            w1_codes[b, a], w1_sc[b, a] = codes, scales
 
-        win = {}
+        def features(kind, b, t):
+            if kind == "h":
+                window = keep.tile([P, S], F32, name=f"h{b}{t}")
+            else:
+                window = e_windows.tile([P, S], F32, name="e")
+            for half in range(HALVES):
+                cols = slice(half * BANK, (half + 1) * BANK)
+                acc = sums.tile([P, BANK], F32, name="acc")
+                for a in range(PASSES):
+                    if kind == "h":
+                        weights = w1_codes[b, a][:, t * P : (t + 1) * P].bitcast(E4M3)
+                        weight_sc = w1_sc[b, a][:, t * P : (t + 1) * P]
+                        moving_sc = v_sc[4 * a :, cols]
+                    else:
+                        weights = w2_w[b][:, a, 2 * t * P : 2 * (t + 1) * P].bitcast(E2M1)
+                        weight_sc = w2_sc[b][:, a, t * P : (t + 1) * P]
+                        moving_sc = (v_sc, v_sc1)[a][:, cols]
+                    nc.tensor.matmul_mx(
+                        out=acc[:],
+                        lhsT=weights,
+                        lhsT_scale=weight_sc,
+                        rhs=v_w[a, half][:].bitcast(E4M3),
+                        rhs_scale=moving_sc,
+                        start=(a == 0),
+                        stop=(a == PASSES - 1),
+                    )
+                nc.scalar.copy(window[:, cols], acc[:])
+            return window
 
-        def feature_bank(rt, kind, half):
-            if (rt, kind) not in win:
-                win[rt, kind] = windows.tile([P, S], F32, name=kind)
-            cols = slice(half * BANK, (half + 1) * BANK)
-            acc = sums.tile([P, BANK], F32, name="acc")
-            for a in range(PASSES):
-                if kind == "h":
-                    weights = w1_codes[rt][:, a * P : (a + 1) * P].bitcast(E4M3)
-                    weight_sc = w1_sc[rt][:, a * P : (a + 1) * P]
-                    moving_sc = v_sc[4 * a :, cols]
+        def places(which, lo, hi):
+            return pos_sb[which][:, lo // LIST_COL : hi // LIST_COL]
+
+
+        def pick_tour(window, b, t):
+            picked = window[:].indirect(pos_sb[TOUR][:])
+            if b * PACK + t < TOURS_ON_SCALAR:
+                nc.scalar.activation(tour[b][:, t, :], picked, ACT.Copy)
+            else:
+                nc.vector.tensor_copy(tour[b][:, t, :], picked)
+
+        def pick_product(prod, b, t, lo, hi):
+            nc.vector.tensor_tensor(
+                prod[:, t, :], h[b, t][:].indirect(places(SAIL, lo, hi)), tour[b][:, t, lo:hi], ALU.mult
+            )
+
+        def pick_products(b, lo, hi):
+            prod = keep.tile([P, PACK, hi - lo], F32, name=f"prod{b}_{lo}")
+            for t in range(PACK):
+                pick_product(prod, b, t, lo, hi)
+            return prod
+
+        def pick_docks(b, lo, hi):
+            dock = keep.tile([P, PACK, hi - lo], F32, name=f"dock{b}_{lo}")
+            for t in range(PACK):
+                picked = h[b, t][:].indirect(places(DOCK, lo, hi))
+                if lo == 0:
+                    nc.scalar.activation(dock[:, t, :], picked, ACT.Copy)
                 else:
-                    weights = w2_w[:, a, 2 * P * rt : 2 * P * (rt + 1)].bitcast(E2M1)
-                    weight_sc = w2_sc[:, a, P * rt : P * (rt + 1)]
-                    moving_sc = (v_sc, v_sc1)[a][:, cols]
-                nc.tensor.matmul_mx(
-                    out=acc[:],
-                    lhsT=weights,
-                    lhsT_scale=weight_sc,
-                    rhs=v_w[half, a].bitcast(E4M3),
-                    rhs_scale=moving_sc,
-                    start=(a == 0),
-                    stop=(a == PASSES - 1),
-                )
-            nc.scalar.copy(win[rt, kind][:, cols], acc[:])
-
-        last = R_TILES - 1
-        prod = {}
-
-        def places(which, mts):
-            return pos_sb[which][:, mts[0] * (P // LIST_COL) : (mts[-1] + 1) * (P // LIST_COL)]
-
-        dock_abs_tiles = [keep.tile([P, M], F32, name=f"dock_abs{i}") for i in range(2)]
-
-        def dock_abs(rt):
-            return dock_abs_tiles[min(rt, last - 1) % 2]
-
-        def pick_dock(rt):
-            dock = picks.tile([P, M], F32, name="dock")
-            nc.vector.tensor_copy(dock[:], win[rt, "h"][:].indirect(pos_sb[DOCK][:]))
+                    nc.vector.tensor_copy(dock[:, t, :], picked)
+            nc.scalar.activation(dock[:], dock[:], ACT.Abs)
             return dock
 
-        def magnitude(dock, rt):
-            nc.scalar.activation(dock_abs(rt)[:], dock[:], ACT.Abs)
+        def quantise(grouped, name):
+            width = grouped.shape[1] // PACK
+            codes = keep.tile([P, width], U32, name=f"{name}_codes", align_bytes=64)
+            scales = keep.tile([P, width], U8, name=f"{name}_sc", align_bytes=64)
+            nc.vector.quantize_mx(out=codes[:].bitcast(E4M3), scales=scales[:], in_=grouped)
+            return codes, scales
 
-        def pick_sail(rt, mts, pool):
-            sail = pool.tile([P, len(mts) * P], F32, name="sail")
-            nc.vector.tensor_copy(sail[:], win[rt, "h"][:].indirect(places(SAIL, mts)))
-            return sail
+        def quantise_z(dock, prod, b, lo, hi):
+            grouped = keep.tile([P, hi - lo, PACK], BF16, name=f"z_grouped{b}_{lo}", align_bytes=64)
+            nc.vector.tensor_tensor(
+                grouped[:].rearrange("p (c i) t -> p c t i", i=4),
+                dock[:].rearrange("p t (c i) -> p c t i", i=4),
+                prod[:].rearrange("p t (c i) -> p c t i", i=4),
+                ALU.add,
+            )
+            return quantise(grouped[:].rearrange("p m t -> p (m t)"), f"z{b}_{lo}")
 
-        def pick_tour_times(sail, rt, mts, pool):
-            product = pool.tile([P, len(mts) * P], F32, name="prod")
-            nc.vector.tensor_tensor(product[:], win[rt, "e"][:].indirect(places(TOUR, mts)), sail[:], ALU.mult)
-            for i, mt in enumerate(mts):
-                prod[rt, mt] = product[:, i * P : (i + 1) * P]
-
-        z_t = [keep.tile([P, M_TILES * PASS], BF16, name=f"z_t{b}", align_bytes=64) for b in range(PASSES)]
-        add_banks = [turns.tile([P, BANK], F32, name=f"add_bank{i}", bufs=1) for i in range(2)]
-
-        def add_turned(rt, mts, bank):
-            b, j = divmod(rt, TILES_PER_PASS)
-            turned = bank[:, : len(mts) * P].rearrange("p (t r) -> p t r", r=P)
-            for i, mt in enumerate(mts):
-                magnitudes = dock_abs(rt)[:, mt * P : (mt + 1) * P]
-                nc.tensor.matmul(turned[:, i, :], magnitudes, ident[:], start=True, stop=False, is_transpose=True)
-                nc.tensor.matmul(turned[:, i, :], prod[rt, mt], ident[:], start=False, stop=True, is_transpose=True)
-            dst = z_t[b][:, mts[0] * PASS : (mts[-1] + 1) * PASS].rearrange(
-                "p (t u j q e) -> p t u j q e", u=2, j=TILES_PER_PASS, q=32, e=2
-            )[:, :, :, j, :, :]
-            nc.scalar.copy(dst, turned.rearrange("p t (q u e) -> p t u q e", u=2, e=2))
-
-        z_codes = [keep.tile([P, M], U32, name=f"z_codes{b}", align_bytes=64) for b in range(PASSES)]
-        z_sc = [keep.tile([P, M], U8, name=f"z_sc{b}", align_bytes=64) for b in range(PASSES)]
-
-        def quantise_z(b, mts):
-            back = turns.tile([P, len(mts), 2, P], F32, name="back")
-            for i, mt in enumerate(mts):
-                words = z_t[b][:, mt * PASS : (mt + 1) * PASS].bitcast(F32)
+        h = {}
+        e = {(b, t): features("e", b, t) for b in range(PASSES) for t in range(PACK)}
+        quantise_w1(0, 0)
+        w1_second = big([P, PASSES * PACK, PASS], F32, "w1_raw1", 2)
+        for a in range(PASSES):
+            load_w1(1, a, w1_second[:, a * PACK : (a + 1) * PACK, :])
+        quantise_w1(0, 1)
+        tour = [big([P, PACK, M], F32, "tour0", 0)]
+        w4_w = big([P, PASSES, N], I32, "w4_w", 1)
+        nc.sync.dma_start(w4_w[:], w4_words.rearrange("a p c i -> p a (c i)").bitcast(I32))
+        for t in range(PACK):
+            h[0, t] = features("h", 0, t)
+            pick_tour(e[0, t], 0, t)
+        quantise_w1(1, 0)
+        quantise_w1(1, 1)
+        tour.append(big([P, PACK, M], F32, "tour1", 2))
+        w4_sc = w1_codes[0, 0][:, : N // 4].bitcast(U8)
+        for q in range(QUADS):
+            nc.sync.dma_start(
+                w1_codes[0, 0][32 * q : 32 * q + 8, : N // 4].bitcast(I32),
+                w4_scales[:, 4 * q : 4 * q + 4, :].bitcast(I32),
+            )
+        for t in range(PACK):
+            pick_tour(e[1, t], 1, t)
+        prod0 = pick_products(0, 0, M)
+        target_sb = big([P, N_TILES, M], F32, "target_sb", 0)
+        nc.sync.dma_start(target_sb[:], target.rearrange("(t p) m -> p t m", p=P))
+        docks0 = []
+        for j in range(PACK):
+            dock = keep.tile([P, M], F32, name=f"dock0{j}")
+            nc.scalar.activation(dock[:], h[0, j][:].indirect(pos_sb[DOCK][:]), ACT.Copy)
+            nc.scalar.activation(dock[:], dock[:], ACT.Abs)
+            docks0.append(dock)
+            h[1, j] = features("h", 1, j)
+        z_t = keep.tile([P, M_TILES * PASS], BF16, name="z_t", align_bytes=64)
+        for j in range(PACK):
+            turned = sums.tile([P, M_TILES, P], F32, name="acc")
+            for mt in range(M_TILES):
+                cols = slice(mt * P, (mt + 1) * P)
+                terms = (docks0[j][:, cols], prod0[:, j, cols])
+                for i, term in enumerate(terms):
+                    nc.tensor.matmul(
+                        turned[:, mt, :], term, ident[:], start=(i == 0), stop=(i == 1), is_transpose=True
+                    )
+            dst = z_t[:].rearrange("p (t u j q e) -> p t u j q e", u=2, j=PACK, q=32, e=2)[:, :, :, j, :, :]
+            nc.scalar.copy(dst, turned[:].rearrange("p t (q u e) -> p t u q e", u=2, e=2))
+        grouped0 = keep.tile([P, M * PACK], BF16, name="z_grouped0", align_bytes=64)
+        for pair in range(M_TILES // 2):
+            back = sums.tile([P, 2, 2, P], F32, name="acc")
+            for i in range(2):
+                words = z_t[:, (2 * pair + i) * PASS : (2 * pair + i + 1) * PASS].bitcast(F32)
                 for u in range(2):
                     nc.tensor.transpose(back[:, i, u, :], words[:, u * P : (u + 1) * P], ident[:])
-            grouped = picks.tile([P, len(mts) * PASS], BF16, name="z_grouped", align_bytes=64)
             nc.scalar.copy(
-                grouped[:].bitcast(F32).rearrange("p (t m u) -> p t m u", t=len(mts), u=2),
+                grouped0[:, 2 * pair * PASS : 2 * (pair + 1) * PASS]
+                .bitcast(F32)
+                .rearrange("p (t m u) -> p t m u", t=2, u=2),
                 back[:].rearrange("p t u m -> p t m u"),
             )
-            cols = slice(mts[0] * P, (mts[-1] + 1) * P)
-            nc.vector.quantize_mx(out=z_codes[b][:, cols].bitcast(E4M3), scales=z_sc[b][:, cols], in_=grouped[:])
+        z0 = quantise(grouped0[:], "z0")
 
-        def load_second_stage():
-            w4_w = w1_ring.tile([P, PASSES, N], I32, name="w4_w", tag="w1_raw", align_bytes=64)
-            nc.sync.dma_start(w4_w[:], w4_words.rearrange("a p c i -> p a (c i)").bitcast(I32))
-            targets = []
-            for half in range(2):
-                part = w1_ring.tile([P, N_TILES, M // 2], F32, name="target_sb", tag="w1_raw", align_bytes=64)
-                cols = slice(half * (M // 2), (half + 1) * (M // 2))
-                nc.sync.dma_start(part[:], target.rearrange("(t p) m -> p t m", p=P)[:, :, cols])
-                targets.extend(part[:, :, i * P : (i + 1) * P] for i in range(M_TILES // 2))
-            spent = w1_codes[2]
-            for q in range(QUADS):
-                nc.sync.dma_start(
-                    spent[32 * q : 32 * q + 4, :].bitcast(I32).rearrange("r (a c) -> r a c", a=PASSES),
-                    w4_scales[:, 4 * q : 4 * q + 4, :].rearrange("a r c -> r a c").bitcast(I32),
-                )
-            return w4_w, spent[:].bitcast(U8), targets
+        def scores(lo, hi, z1):
+            width = hi - lo
+            per_bank = BANK // width
+            banks = []
+            for first in range(0, N_TILES, per_bank):
+                y = sums.tile([P, per_bank, width], F32, name="acc")
+                for b in range(PASSES):
+                    codes, scales = (z0[0][:, lo:hi], z0[1][:, lo:hi]) if b == 0 else (z1[0][:], z1[1][:])
+                    for i in range(per_bank):
+                        cols = slice((first + i) * P, (first + i + 1) * P)
+                        nc.tensor.matmul_mx(
+                            out=y[:, i, :],
+                            lhsT=w4_w[:, b, cols].bitcast(E4M3),
+                            lhsT_scale=w4_sc[4 * b :, cols],
+                            rhs=codes.bitcast(E4M3),
+                            rhs_scale=scales,
+                            start=(b == 0 and i == 0),
+                            stop=(b == PASSES - 1 and i == per_bank - 1),
+                        )
+                banks.append((y, first, per_bank))
+            return banks
 
-        def scores(y, b, mt):
-            cols = slice(mt * P, (mt + 1) * P)
-            for nt in range(N_TILES):
-                nc.tensor.matmul_mx(
-                    out=y[:, nt, :],
-                    lhsT=w4_w[:, b, nt * P : (nt + 1) * P].bitcast(E4M3),
-                    lhsT_scale=w4_sc[:, b * N + nt * P : b * N + (nt + 1) * P],
-                    rhs=z_codes[b][:, cols].bitcast(E4M3),
-                    rhs_scale=z_sc[b][:, cols],
-                    start=(b == 0 and nt == 0),
-                    stop=(b == PASSES - 1 and nt == N_TILES - 1),
-                )
-
-        def residual(y, mt):
-            res = ends.tile([P, N_TILES, P], F32, name="res")
-            sq = ends.tile([P, N_TILES, P], F32, name="sq")
-            nc.vector.tensor_tensor(res[:], targets[mt], y[:], ALU.subtract)
+        def finish(y, first, count, lo, hi):
+            tiles = slice(first, first + count)
+            res = ring.tile([P, count, hi - lo], F32, name="res", bufs=4)
+            sq = ring.tile([P, count, hi - lo], F32, name="sq", bufs=4)
+            nc.vector.tensor_tensor(res[:], target_sb[:, tiles, lo:hi], y[:], ALU.subtract)
             nc.scalar.activation(sq[:], res[:], ACT.Square)
-            return res, sq
+            nc.vector.tensor_tensor(sq[:], sq[:], res[:], ALU.mult)
+            nc.sync.dma_start(out.rearrange("(t p) m -> p t m", p=P)[:, tiles, lo:hi], sq[:])
 
-        def finish(res, sq, mt):
-            cols = slice(mt * P, (mt + 1) * P)
-            cube = ends.tile([P, N_TILES, P], F32, name="cube")
-            nc.vector.tensor_tensor(cube[:], sq[:], res[:], ALU.mult)
-            nc.sync.dma_start(out.rearrange("(t p) m -> p t m", p=P)[:, :, cols], cube[:])
-
-        all_mts = list(range(M_TILES))
-
-        def banks(rt):
-            kinds = ("h", "e") if rt < last else ("e", "h")
-            return [(rt, kind, half) for kind in kinds for half in range(HALVES)]
-
-        quantise_w1(0)
-        quantise_w1(1)
-        load_w1(3)
-        for job in banks(0):
-            feature_bank(*job)
-        quantise_w1(2)
-        for job in banks(1)[:HALVES]:
-            feature_bank(*job)
-        quantise_w1(3)
-        load_w1(4)
-        for job in banks(1)[HALVES:]:
-            feature_bank(*job)
-
-        for rt in range(last):
-            sail = pick_sail(rt, all_mts, picks)
-            dock = pick_dock(rt)
-            pick_tour_times(sail, rt, all_mts, picks)
-            between = []
-            if rt >= 1:
-                between.append(lambda: add_turned(rt - 1, all_mts, add_banks[0]))
-            between.append(lambda: magnitude(dock, rt))
-            if rt + W1_AHEAD < R_TILES:
-                between.append(lambda: quantise_w1(rt + W1_AHEAD))
-            if rt == TILES_PER_PASS:
-                between.append(lambda: quantise_z(0, all_mts[:2]))
-                between.append(lambda: quantise_z(0, all_mts[2:]))
-            jobs = banks(rt + FEATURES_AHEAD) if rt + FEATURES_AHEAD < R_TILES else []
-            for i in range(max(len(jobs), len(between))):
-                if i < len(jobs):
-                    feature_bank(*jobs[i])
-                if i < len(between):
-                    between[i]()
-            if rt == 1:
-                w4_w, w4_sc, targets = load_second_stage()
-
-        ys = [sums.tile([P, N_TILES, P], F32, name="acc") for mt in all_mts]
-        dock = pick_dock(last)
-        add_turned(last - 1, all_mts[:2], add_banks[1])
-        add_turned(last - 1, all_mts[2:], add_banks[0])
-        magnitude(dock, last)
-        sails = [pick_sail(last, [0], tail)]
-        for mt in all_mts:
-            if mt + 1 < M_TILES:
-                sails.append(pick_sail(last, [mt + 1], tail))
-            pick_tour_times(sails[mt], last, [mt], tail)
-        for mt in all_mts:
-            scores(ys[mt], 0, mt)
-        for step in range(M_TILES + 2):
-            if step < M_TILES:
-                add_turned(last, [step], add_banks[(step + 1) % 2])
-            if 0 <= step - 1 < M_TILES:
-                quantise_z(1, [step - 1])
-            if 0 <= step - 2 < M_TILES:
-                scores(ys[step - 2], 1, step - 2)
-        residuals = [residual(ys[mt], mt) for mt in all_mts]
-        for mt in all_mts:
-            finish(*residuals[mt], mt)
+        waiting = []
+        for lo, hi in PIECES:
+            prod = pick_products(1, lo, hi)
+            z1 = quantise_z(pick_docks(1, lo, hi), prod, 1, lo, hi)
+            for job in waiting:
+                finish(*job)
+            waiting = [(*bank, lo, hi) for bank in scores(lo, hi, z1)]
+        for job in waiting:
+            finish(*job)

@@ -28,7 +28,6 @@ LIST_COL = 16
 N_TILES = N // P
 M_TILES = M // P
 PIECES = [(0, 256), (256, 384), (384, 512)]
-TOURS_ON_SCALAR = 0
 
 
 def tile_list_cruise_slot_corrections_kernel(
@@ -174,7 +173,7 @@ def tile_list_cruise_slot_corrections_kernel(
 
         def pick_tour(window, b, t):
             picked = window[:].indirect(pos_sb[TOUR][:])
-            if b * PACK + t < TOURS_ON_SCALAR:
+            if b == 1:
                 nc.scalar.activation(tour[b][:, t, :], picked, ACT.Copy)
             else:
                 nc.vector.tensor_copy(tour[b][:, t, :], picked)
@@ -194,10 +193,7 @@ def tile_list_cruise_slot_corrections_kernel(
             dock = keep.tile([P, PACK, hi - lo], F32, name=f"dock{b}_{lo}")
             for t in range(PACK):
                 picked = h[b, t][:].indirect(places(DOCK, lo, hi))
-                if lo == 0:
-                    nc.scalar.activation(dock[:, t, :], picked, ACT.Copy)
-                else:
-                    nc.vector.tensor_copy(dock[:, t, :], picked)
+                nc.scalar.activation(dock[:, t, :], picked, ACT.Copy)
             nc.scalar.activation(dock[:], dock[:], ACT.Abs)
             return dock
 
@@ -233,7 +229,7 @@ def tile_list_cruise_slot_corrections_kernel(
             pick_tour(e[0, t], 0, t)
         quantise_w1(1, 0)
         quantise_w1(1, 1)
-        tour.append(big([P, PACK, M], F32, "tour1", 2))
+        tour.append(keep.tile([P, PACK, M], F32, name="tour1"))
         w4_sc = w1_codes[0, 0][:, : N // 4].bitcast(U8)
         for q in range(QUADS):
             nc.sync.dma_start(
@@ -242,28 +238,31 @@ def tile_list_cruise_slot_corrections_kernel(
             )
         for t in range(PACK):
             pick_tour(e[1, t], 1, t)
-        prod0 = pick_products(0, 0, M)
-        target_sb = big([P, N_TILES, M], F32, "target_sb", 0)
-        nc.sync.dma_start(target_sb[:], target.rearrange("(t p) m -> p t m", p=P))
-        docks0 = []
-        for j in range(PACK):
-            dock = keep.tile([P, M], F32, name=f"dock0{j}")
-            nc.scalar.activation(dock[:], h[0, j][:].indirect(pos_sb[DOCK][:]), ACT.Copy)
-            nc.scalar.activation(dock[:], dock[:], ACT.Abs)
-            docks0.append(dock)
-            h[1, j] = features("h", 1, j)
+        h[1, 0] = features("h", 1, 0)
+        prod0 = keep.tile([P, PACK, M], F32, name="prod0")
         z_t = keep.tile([P, M_TILES * PASS], BF16, name="z_t", align_bytes=64)
         for j in range(PACK):
+            if j + 1 < PACK:
+                h[1, j + 1] = features("h", 1, j + 1)
+            else:
+                first_docks = pick_docks(1, *PIECES[0])
+            dock = ring.tile([P, M], F32, name="dock0", bufs=4)
+            nc.vector.tensor_copy(dock[:], h[0, j][:].indirect(pos_sb[DOCK][:]))
+            pick_product(prod0, 0, j, 0, M)
+            lift = ring.tile([P, M], F32, name="lift", bufs=4)
+            nc.vector.tensor_scalar(lift[:], dock[:], -2.0, 0.0, ALU.mult, ALU.max)
             turned = sums.tile([P, M_TILES, P], F32, name="acc")
             for mt in range(M_TILES):
                 cols = slice(mt * P, (mt + 1) * P)
-                terms = (docks0[j][:, cols], prod0[:, j, cols])
+                terms = (dock[:, cols], lift[:, cols], prod0[:, j, cols])
                 for i, term in enumerate(terms):
                     nc.tensor.matmul(
-                        turned[:, mt, :], term, ident[:], start=(i == 0), stop=(i == 1), is_transpose=True
+                        turned[:, mt, :], term, ident[:], start=(i == 0), stop=(i == 2), is_transpose=True
                     )
             dst = z_t[:].rearrange("p (t u j q e) -> p t u j q e", u=2, j=PACK, q=32, e=2)[:, :, :, j, :, :]
             nc.scalar.copy(dst, turned[:].rearrange("p t (q u e) -> p t u q e", u=2, e=2))
+        target_sb = big([P, N_TILES, M], F32, "target_sb", 0)
+        nc.sync.dma_start(target_sb[:], target.rearrange("(t p) m -> p t m", p=P))
         grouped0 = keep.tile([P, M * PACK], BF16, name="z_grouped0", align_bytes=64)
         for pair in range(M_TILES // 2):
             back = sums.tile([P, 2, 2, P], F32, name="acc")
@@ -301,21 +300,27 @@ def tile_list_cruise_slot_corrections_kernel(
                 banks.append((y, first, per_bank))
             return banks
 
-        def finish(y, first, count, lo, hi):
-            tiles = slice(first, first + count)
-            res = ring.tile([P, count, hi - lo], F32, name="res", bufs=4)
-            sq = ring.tile([P, count, hi - lo], F32, name="sq", bufs=4)
-            nc.vector.tensor_tensor(res[:], target_sb[:, tiles, lo:hi], y[:], ALU.subtract)
+        def residual(y, first, count, lo, hi):
+            res = ring.tile([P, count, hi - lo], F32, name="res", bufs=5)
+            sq = ring.tile([P, count, hi - lo], F32, name="sq", bufs=5)
+            nc.vector.tensor_tensor(res[:], target_sb[:, first : first + count, lo:hi], y, ALU.subtract)
             nc.scalar.activation(sq[:], res[:], ACT.Square)
-            nc.vector.tensor_tensor(sq[:], sq[:], res[:], ALU.mult)
-            nc.sync.dma_start(out.rearrange("(t p) m -> p t m", p=P)[:, tiles, lo:hi], sq[:])
+            return res, sq, first, count, lo, hi
 
-        waiting = []
+        def finish(res, sq, first, count, lo, hi):
+            nc.vector.tensor_tensor(sq[:], sq[:], res[:], ALU.mult)
+            nc.sync.dma_start(out.rearrange("(t p) m -> p t m", p=P)[:, first : first + count, lo:hi], sq[:])
+
+        banks, squared = [], []
         for lo, hi in PIECES:
             prod = pick_products(1, lo, hi)
-            z1 = quantise_z(pick_docks(1, lo, hi), prod, 1, lo, hi)
-            for job in waiting:
+            z1 = quantise_z(first_docks if lo == 0 else pick_docks(1, lo, hi), prod, 1, lo, hi)
+            for job in squared:
                 finish(*job)
-            waiting = [(*bank, lo, hi) for bank in scores(lo, hi, z1)]
-        for job in waiting:
+            squared = [residual(*job) for job in banks]
+            banks = [(y[:], first, count, lo, hi) for y, first, count in scores(lo, hi, z1)]
+        y, first, count, lo, hi = banks[0]
+        half = count // 2
+        last = [residual(y[:, i * half : (i + 1) * half, :], i * half, half, lo, hi) for i in range(2)]
+        for job in squared + last:
             finish(*job)

@@ -52,17 +52,12 @@ def tile_list_cruise_slot_corrections_kernel(
         w2_sc_raw = keep.tile([P, PASSES * H], U8, name="w2_sc_raw", align_bytes=64)
         nc.vector.memset(w2_sc_raw[:].bitcast(I32), 0)
         v_sc1 = keep.tile([P, S], U8, name="v_sc1", align_bytes=64)
-        nc.vector.memset(v_sc1[:].bitcast(I32), 0)
-        for q in range(QUADS):
-            nc.gpsimd.dma_start(
-                w2_sc_raw[32 * q : 32 * q + 4, :].bitcast(I32).rearrange("r (a c) -> r a c", a=PASSES),
-                w2_scales[:, 4 * q : 4 * q + 4, :].rearrange("a r c -> r a c").bitcast(I32),
-            )
+        nc.gpsimd.memset(v_sc1[:].bitcast(I32), 0)
 
         tab_w = [big([P, T], I32, f"tab_w{a}", a) for a in range(PASSES)]
         ident = keep.tile([P, P], F32, name="ident")
         make_identity(nc, ident[:])
-        w2_raw = keep.tile([P, PASSES, 2 * H], U8, name="w2_raw", align_bytes=64)
+        w2_raw = [keep.tile([P, PASSES, 2 * PASS], U8, name=f"w2_raw{b}", align_bytes=64) for b in range(PASSES)]
         w1_raw = {}
 
         def load_table_words(a):
@@ -81,9 +76,16 @@ def tile_list_cruise_slot_corrections_kernel(
                 tab_sc[32 * q : 32 * q + 8, :].bitcast(I32), tab_scales[:, 4 * q : 4 * q + 4, :].bitcast(I32)
             )
         load_table_words(0)
-        load_table_words(1)
-        nc.sync.dma_start(w2_raw[:].bitcast(I32), w2_words.rearrange("a p c -> p a c").bitcast(I32))
+        for q in range(QUADS):
+            nc.sync.dma_start(
+                w2_sc_raw[32 * q : 32 * q + 4, :].bitcast(I32).rearrange("r (a c) -> r a c", a=PASSES),
+                w2_scales[:, 4 * q : 4 * q + 4, :].rearrange("a r c -> r a c").bitcast(I32),
+            )
         nc.sync.dma_start(pos_sb[DOCK][:], pos1)
+        load_table_words(1)
+        w2_halves = w2_words.rearrange("a p (b c) -> b p a c", b=PASSES)
+        for b in range(PASSES):
+            nc.sync.dma_start(w2_raw[b][:].bitcast(I32), w2_halves[b].bitcast(I32))
 
         v_sc = keep.tile([P, S], U8, name="v_sc", align_bytes=64)
         nc.vector.tensor_copy(v_sc[:], tab_sc[:].indirect(offs_sb[:]))
@@ -94,28 +96,29 @@ def tile_list_cruise_slot_corrections_kernel(
         load_w1(0, 0, big([P, PACK, PASS], F32, "w1_raw00", 2)[:])
         v_w = {}
 
-        def gather_words(a):
-            for half in range(HALVES):
-                entries = offs_sb[:, half * (BANK // LIST_COL) : (half + 1) * (BANK // LIST_COL)]
-                words = keep.tile([P, BANK], U32, name=f"v_w{a}{half}", align_bytes=64)
-                nc.vector.tensor_copy(words[:], tab_w[a][:].bitcast(U32).indirect(entries))
-                v_w[a, half] = words
+        def gather_words(a, pieces):
+            words = keep.tile([P, S], U32, name=f"v_w{a}", align_bytes=64)
+            step = S // pieces
+            for lo in range(0, S, step):
+                entries = offs_sb[:, lo // LIST_COL : (lo + step) // LIST_COL]
+                nc.vector.tensor_copy(words[:, lo : lo + step], tab_w[a][:].bitcast(U32).indirect(entries))
+            v_w[a] = words
 
-        gather_words(0)
+        gather_words(0, 1)
         load_w1(0, 1, big([P, PACK, PASS], F32, "w1_raw01", 0)[:])
-        gather_words(1)
+        gather_words(1, HALVES)
 
         dealt = big([P, 3 * H], U8, "w2_dealt", 1)
         nc.vector.tensor_copy(
             dealt[:, : 2 * H].bitcast(U16).rearrange("p (a t q) -> p a q t", a=PASSES, t=PACK),
-            w2_raw[:, :, H:].bitcast(U16).rearrange("p a (q t) -> p a q t", t=PACK),
+            w2_raw[1][:].bitcast(U16).rearrange("p a (q t) -> p a q t", t=PACK),
         )
         w2_sc_by_pass = w2_sc_raw[:].rearrange("p (a c) -> p a c", a=PASSES)
         nc.vector.tensor_copy(
             dealt[:, 2 * H :].rearrange("p (a t q) -> p a q t", a=PASSES, t=PACK),
             w2_sc_by_pass[:, :, PASS:].rearrange("p a (q t) -> p a q t", t=PACK),
         )
-        w2_w = [w2_raw, dealt[:, : 2 * H].rearrange("p (a c) -> p a c", a=PASSES)]
+        w2_w = [w2_raw[0], dealt[:, : 2 * H].rearrange("p (a c) -> p a c", a=PASSES)]
         w2_sc = [w2_sc_by_pass, dealt[:, 2 * H :].rearrange("p (a c) -> p a c", a=PASSES)]
 
         w1_codes, w1_sc = {}, {}
@@ -159,7 +162,7 @@ def tile_list_cruise_slot_corrections_kernel(
                         out=acc[:],
                         lhsT=weights,
                         lhsT_scale=weight_sc,
-                        rhs=v_w[a, half][:].bitcast(E4M3),
+                        rhs=v_w[a][:, cols].bitcast(E4M3),
                         rhs_scale=moving_sc,
                         start=(a == 0),
                         stop=(a == PASSES - 1),
@@ -209,7 +212,7 @@ def tile_list_cruise_slot_corrections_kernel(
             nc.vector.tensor_tensor(
                 grouped[:].rearrange("p (c i) t -> p c t i", i=4),
                 dock[:].rearrange("p t (c i) -> p c t i", i=4),
-                prod[:].rearrange("p t (c i) -> p c t i", i=4),
+                prod.rearrange("p t (c i) -> p c t i", i=4),
                 ALU.add,
             )
             return quantise(grouped[:].rearrange("p m t -> p (m t)"), f"z{b}_{lo}")
@@ -311,10 +314,10 @@ def tile_list_cruise_slot_corrections_kernel(
             nc.vector.tensor_tensor(sq[:], sq[:], res[:], ALU.mult)
             nc.sync.dma_start(out.rearrange("(t p) m -> p t m", p=P)[:, first : first + count, lo:hi], sq[:])
 
+        prod1 = pick_products(1, 0, M)
         banks, squared = [], []
         for lo, hi in PIECES:
-            prod = pick_products(1, lo, hi)
-            z1 = quantise_z(first_docks if lo == 0 else pick_docks(1, lo, hi), prod, 1, lo, hi)
+            z1 = quantise_z(first_docks if lo == 0 else pick_docks(1, lo, hi), prod1[:, :, lo:hi], 1, lo, hi)
             for job in squared:
                 finish(*job)
             squared = [residual(*job) for job in banks]

@@ -48,11 +48,16 @@ def tile_list_cruise_slot_corrections_kernel(
         DOCK, TOUR, SAIL = 0, 1, 2
 
         tab_sc = big([P, T], U8, "tab_sc", 2)
-        nc.gpsimd.memset(tab_sc[:].bitcast(I32), 0)
+        nc.vector.memset(tab_sc[:].bitcast(I32), 0)
         w2_sc_raw = keep.tile([P, PASSES * H], U8, name="w2_sc_raw", align_bytes=64)
-        nc.vector.memset(w2_sc_raw[:].bitcast(I32), 0)
+        nc.gpsimd.memset(w2_sc_raw[:].bitcast(I32), 0)
+        for q in range(QUADS):
+            nc.gpsimd.dma_start(
+                w2_sc_raw[32 * q : 32 * q + 4, :].bitcast(I32).rearrange("r (a c) -> r a c", a=PASSES),
+                w2_scales[:, 4 * q : 4 * q + 4, :].rearrange("a r c -> r a c").bitcast(I32),
+            )
         v_sc1 = keep.tile([P, S], U8, name="v_sc1", align_bytes=64)
-        nc.gpsimd.memset(v_sc1[:].bitcast(I32), 0)
+        nc.vector.memset(v_sc1[:].bitcast(I32), 0)
 
         tab_w = [big([P, T], I32, f"tab_w{a}", a) for a in range(PASSES)]
         ident = keep.tile([P, P], F32, name="ident")
@@ -76,16 +81,11 @@ def tile_list_cruise_slot_corrections_kernel(
                 tab_sc[32 * q : 32 * q + 8, :].bitcast(I32), tab_scales[:, 4 * q : 4 * q + 4, :].bitcast(I32)
             )
         load_table_words(0)
-        for q in range(QUADS):
-            nc.sync.dma_start(
-                w2_sc_raw[32 * q : 32 * q + 4, :].bitcast(I32).rearrange("r (a c) -> r a c", a=PASSES),
-                w2_scales[:, 4 * q : 4 * q + 4, :].rearrange("a r c -> r a c").bitcast(I32),
-            )
-        nc.sync.dma_start(pos_sb[DOCK][:], pos1)
         load_table_words(1)
         w2_halves = w2_words.rearrange("a p (b c) -> b p a c", b=PASSES)
         for b in range(PASSES):
             nc.sync.dma_start(w2_raw[b][:].bitcast(I32), w2_halves[b].bitcast(I32))
+        nc.sync.dma_start(pos_sb[DOCK][:], pos1)
 
         v_sc = keep.tile([P, S], U8, name="v_sc", align_bytes=64)
         nc.vector.tensor_copy(v_sc[:], tab_sc[:].indirect(offs_sb[:]))

@@ -110,13 +110,13 @@ def tile_list_cruise_slot_corrections_kernel(
 
         dealt = big([P, 3 * H], U8, "w2_dealt", 1)
         nc.vector.tensor_copy(
-            dealt[:, : 2 * H].bitcast(U16).rearrange("p (a t q) -> p a q t", a=PASSES, t=PACK),
-            w2_raw[1][:].bitcast(U16).rearrange("p a (q t) -> p a q t", t=PACK),
+            dealt[:, : 2 * H].bitcast(U16).rearrange("p (a t q) -> p a t q", a=PASSES, t=PACK),
+            w2_raw[1][:].bitcast(U16).rearrange("p a (q t) -> p a t q", t=PACK),
         )
         w2_sc_by_pass = w2_sc_raw[:].rearrange("p (a c) -> p a c", a=PASSES)
         nc.vector.tensor_copy(
-            dealt[:, 2 * H :].rearrange("p (a t q) -> p a q t", a=PASSES, t=PACK),
-            w2_sc_by_pass[:, :, PASS:].rearrange("p a (q t) -> p a q t", t=PACK),
+            dealt[:, 2 * H :].rearrange("p (a t q) -> p a t q", a=PASSES, t=PACK),
+            w2_sc_by_pass[:, :, PASS:].rearrange("p a (q t) -> p a t q", t=PACK),
         )
         w2_w = [w2_raw[0], dealt[:, : 2 * H].rearrange("p (a c) -> p a c", a=PASSES)]
         w2_sc = [w2_sc_by_pass, dealt[:, 2 * H :].rearrange("p (a c) -> p a c", a=PASSES)]
@@ -132,7 +132,8 @@ def tile_list_cruise_slot_corrections_kernel(
                 )
             else:
                 nc.vector.tensor_copy(
-                    grouped[:].rearrange("p (t q) j -> p q j t", t=PACK), raw.rearrange("p j (q t) -> p q j t", t=PACK)
+                    grouped[:].rearrange("p (u e q) j -> p u q j e", u=2, e=2),
+                    raw.rearrange("p j (q u e) -> p u q j e", u=2, e=2),
                 )
             codes = keep.tile([P, PASS], U32, name=f"w1_codes{b}{a}", align_bytes=64)
             scales = keep.tile([P, PASS], U8, name=f"w1_sc{b}{a}", align_bytes=64)

@@ -127,9 +127,15 @@ def tile_list_cruise_slot_corrections_kernel(
             grouped = ring.tile([P, PASS, PACK], BF16, name="w1_grouped", align_bytes=64)
             raw = w1_raw[b, a]
             if b == 0:
-                nc.vector.tensor_copy(
-                    grouped[:].rearrange("p (c i) j -> p c j i", i=4), raw.rearrange("p j (c i) -> p c j i", i=4)
-                )
+                for lo in range(0, PASS, P):
+                    nc.gpsimd.tensor_scalar(
+                        grouped[:, lo : lo + P, :].rearrange("p (c i) j -> p c j i", i=4),
+                        raw[:, :, lo : lo + P].rearrange("p j (c i) -> p c j i", i=4),
+                        1.0,
+                        0.0,
+                        ALU.mult,
+                        ALU.add,
+                    )
             else:
                 nc.vector.tensor_copy(
                     grouped[:].rearrange("p (u e q) j -> p u q j e", u=2, e=2),
@@ -177,7 +183,7 @@ def tile_list_cruise_slot_corrections_kernel(
 
         def pick_tour(window, b, t):
             picked = window[:].indirect(pos_sb[TOUR][:])
-            if b == 1:
+            if b == 1 and t > 1:
                 nc.scalar.activation(tour[b][:, t, :], picked, ACT.Copy)
             else:
                 nc.vector.tensor_copy(tour[b][:, t, :], picked)
@@ -220,17 +226,18 @@ def tile_list_cruise_slot_corrections_kernel(
 
         h = {}
         e = {(b, t): features("e", b, t) for b in range(PASSES) for t in range(PACK)}
+        tour = [keep.tile([P, PACK, M], F32, name="tour0")]
+        for t in range(PACK):
+            pick_tour(e[0, t], 0, t)
         quantise_w1(0, 0)
         w1_second = big([P, PASSES * PACK, PASS], F32, "w1_raw1", 2)
         for a in range(PASSES):
             load_w1(1, a, w1_second[:, a * PACK : (a + 1) * PACK, :])
         quantise_w1(0, 1)
-        tour = [big([P, PACK, M], F32, "tour0", 0)]
         w4_w = big([P, PASSES, N], I32, "w4_w", 1)
         nc.sync.dma_start(w4_w[:], w4_words.rearrange("a p c i -> p a (c i)").bitcast(I32))
         for t in range(PACK):
             h[0, t] = features("h", 0, t)
-            pick_tour(e[0, t], 0, t)
         quantise_w1(1, 0)
         quantise_w1(1, 1)
         tour.append(keep.tile([P, PACK, M], F32, name="tour1"))

@@ -27,6 +27,7 @@ QUADS = 4
 LIST_COL = 16
 N_TILES = N // P
 M_TILES = M // P
+DOCKS_ON_VECTOR = 1
 PIECES = [(0, 256), (256, 384), (384, 512)]
 
 
@@ -62,7 +63,7 @@ def tile_list_cruise_slot_corrections_kernel(
         tab_w = [big([P, T], I32, f"tab_w{a}", a) for a in range(PASSES)]
         ident = keep.tile([P, P], F32, name="ident")
         make_identity(nc, ident[:])
-        w2_raw = [keep.tile([P, PASSES, 2 * PASS], U8, name=f"w2_raw{b}", align_bytes=64) for b in range(PASSES)]
+        w2_raw = [keep.tile([P, PASSES, 2 * PASS], U8, name=f"w2_raw{b}", tag=f"w2_raw{b}", align_bytes=64) for b in range(PASSES)]
         w1_raw = {}
 
         def load_table_words(a):
@@ -108,45 +109,50 @@ def tile_list_cruise_slot_corrections_kernel(
         load_w1(0, 1, big([P, PACK, PASS], F32, "w1_raw01", 0)[:])
         gather_words(1, HALVES)
 
-        dealt = big([P, 3 * H], U8, "w2_dealt", 1)
+        dealt_w = keep.tile([P, PASSES, 2 * PASS], U8, name="w2_dealt", align_bytes=64)
         nc.vector.tensor_copy(
-            dealt[:, : 2 * H].bitcast(U16).rearrange("p (a t q) -> p a t q", a=PASSES, t=PACK),
+            dealt_w[:].bitcast(U16).rearrange("p a (t q) -> p a t q", t=PACK),
             w2_raw[1][:].bitcast(U16).rearrange("p a (q t) -> p a t q", t=PACK),
         )
         w2_sc_by_pass = w2_sc_raw[:].rearrange("p (a c) -> p a c", a=PASSES)
-        nc.vector.tensor_copy(
-            dealt[:, 2 * H :].rearrange("p (a t q) -> p a t q", a=PASSES, t=PACK),
+        dealt_sc = keep.tile([P, PASSES, PASS], U8, name="w2_sc_dealt", align_bytes=64)
+        nc.gpsimd.tensor_copy(
+            dealt_sc[:].rearrange("p a (t q) -> p a t q", t=PACK),
             w2_sc_by_pass[:, :, PASS:].rearrange("p a (q t) -> p a t q", t=PACK),
         )
-        w2_w = [w2_raw[0], dealt[:, : 2 * H].rearrange("p (a c) -> p a c", a=PASSES)]
-        w2_sc = [w2_sc_by_pass, dealt[:, 2 * H :].rearrange("p (a c) -> p a c", a=PASSES)]
+        w2_w = [w2_raw[0], dealt_w]
+        w2_sc = [w2_sc_by_pass, dealt_sc]
+        w1_second = big([P, PASSES * PACK, PASS], F32, "w1_raw1", 1)
+        for a in range(PASSES):
+            load_w1(1, a, w1_second[:, a * PACK : (a + 1) * PACK, :])
 
         w1_codes, w1_sc = {}, {}
 
-        def quantise_w1(b, a):
-            grouped = ring.tile([P, PASS, PACK], BF16, name="w1_grouped", align_bytes=64)
+        def group_w1(b, a, grouped):
             raw = w1_raw[b, a]
-            if b == 0:
-                for lo in range(0, PASS, P):
-                    nc.gpsimd.tensor_scalar(
-                        grouped[:, lo : lo + P, :].rearrange("p (c i) j -> p c j i", i=4),
-                        raw[:, :, lo : lo + P].rearrange("p j (c i) -> p c j i", i=4),
-                        1.0,
-                        0.0,
-                        ALU.mult,
-                        ALU.add,
-                    )
-            else:
-                nc.vector.tensor_copy(
-                    grouped[:].rearrange("p (u e q) j -> p u q j e", u=2, e=2),
-                    raw.rearrange("p j (q u e) -> p u q j e", u=2, e=2),
-                )
-            codes = keep.tile([P, PASS], U32, name=f"w1_codes{b}{a}", align_bytes=64)
-            scales = keep.tile([P, PASS], U8, name=f"w1_sc{b}{a}", align_bytes=64)
+            for piece in range(4):
+                if b == 0:
+                    cols = slice(piece * P, (piece + 1) * P)
+                    dst = grouped[:, cols, :].rearrange("p (c i) j -> p c j i", i=4)
+                    src = raw[:, :, cols].rearrange("p j (c i) -> p c j i", i=4)
+                else:
+                    u, rows = piece // 2, slice(piece % 2 * (P // 2), (piece % 2 + 1) * (P // 2))
+                    dst = grouped.rearrange("p (u e q) j -> p u q j e", u=2, e=2)[:, u, rows]
+                    src = raw.rearrange("p j (q u e) -> p u q j e", u=2, e=2)[:, u, rows]
+                nc.gpsimd.tensor_scalar(dst, src, 1.0, 0.0, ALU.mult, ALU.add)
+
+        def quantise_w1(b):
+            grouped = ring.tile([P, PASSES * PASS, PACK], BF16, name="w1_grouped", tag="w1_grouped", align_bytes=64)
+            for a in range(PASSES):
+                group_w1(b, a, grouped[:, a * PASS : (a + 1) * PASS, :])
+            codes = keep.tile([P, PASSES, PASS], U32, name=f"w1_codes{b}", align_bytes=64)
+            scales = keep.tile([P, PASSES, PASS], U8, name=f"w1_sc{b}", align_bytes=64)
             nc.vector.quantize_mx(
-                out=codes[:].bitcast(E4M3), scales=scales[:], in_=grouped[:].rearrange("p c j -> p (c j)")
+                out=codes[:].rearrange("p a c -> p (a c)").bitcast(E4M3),
+                scales=scales[:].rearrange("p a c -> p (a c)"),
+                in_=grouped[:].rearrange("p c j -> p (c j)"),
             )
-            w1_codes[b, a], w1_sc[b, a] = codes, scales
+            w1_codes[b], w1_sc[b] = codes, scales
 
         def features(kind, b, t):
             if kind == "h":
@@ -158,8 +164,8 @@ def tile_list_cruise_slot_corrections_kernel(
                 acc = sums.tile([P, BANK], F32, name="acc")
                 for a in range(PASSES):
                     if kind == "h":
-                        weights = w1_codes[b, a][:, t * P : (t + 1) * P].bitcast(E4M3)
-                        weight_sc = w1_sc[b, a][:, t * P : (t + 1) * P]
+                        weights = w1_codes[b][:, a, t * P : (t + 1) * P].bitcast(E4M3)
+                        weight_sc = w1_sc[b][:, a, t * P : (t + 1) * P]
                         moving_sc = v_sc[4 * a :, cols]
                     else:
                         weights = w2_w[b][:, a, 2 * t * P : 2 * (t + 1) * P].bitcast(E2M1)
@@ -182,11 +188,7 @@ def tile_list_cruise_slot_corrections_kernel(
 
 
         def pick_tour(window, b, t):
-            picked = window[:].indirect(pos_sb[TOUR][:])
-            if b == 1 and t > 1:
-                nc.scalar.activation(tour[b][:, t, :], picked, ACT.Copy)
-            else:
-                nc.vector.tensor_copy(tour[b][:, t, :], picked)
+            nc.vector.tensor_copy(tour[b][:, t, :], window[:].indirect(pos_sb[TOUR][:]))
 
         def pick_product(prod, b, t, lo, hi):
             nc.vector.tensor_tensor(
@@ -199,11 +201,14 @@ def tile_list_cruise_slot_corrections_kernel(
                 pick_product(prod, b, t, lo, hi)
             return prod
 
-        def pick_docks(b, lo, hi):
-            dock = keep.tile([P, PACK, hi - lo], F32, name=f"dock{b}_{lo}")
+        def pick_docks(lo, hi, on_vector):
+            dock = keep.tile([P, PACK, hi - lo], F32, name=f"dock1_{lo}")
             for t in range(PACK):
-                picked = h[b, t][:].indirect(places(DOCK, lo, hi))
-                nc.scalar.activation(dock[:, t, :], picked, ACT.Copy)
+                picked = h[1, t][:].indirect(places(DOCK, lo, hi))
+                if on_vector:
+                    nc.vector.tensor_copy(dock[:, t, :], picked)
+                else:
+                    nc.scalar.activation(dock[:, t, :], picked, ACT.Copy)
             nc.scalar.activation(dock[:], dock[:], ACT.Abs)
             return dock
 
@@ -218,7 +223,7 @@ def tile_list_cruise_slot_corrections_kernel(
             grouped = keep.tile([P, hi - lo, PACK], BF16, name=f"z_grouped{b}_{lo}", align_bytes=64)
             nc.vector.tensor_tensor(
                 grouped[:].rearrange("p (c i) t -> p c t i", i=4),
-                dock[:].rearrange("p t (c i) -> p c t i", i=4),
+                dock.rearrange("p t (c i) -> p c t i", i=4),
                 prod.rearrange("p t (c i) -> p c t i", i=4),
                 ALU.add,
             )
@@ -229,39 +234,43 @@ def tile_list_cruise_slot_corrections_kernel(
         tour = [keep.tile([P, PACK, M], F32, name="tour0")]
         for t in range(PACK):
             pick_tour(e[0, t], 0, t)
-        quantise_w1(0, 0)
-        w1_second = big([P, PASSES * PACK, PASS], F32, "w1_raw1", 2)
-        for a in range(PASSES):
-            load_w1(1, a, w1_second[:, a * PACK : (a + 1) * PACK, :])
-        quantise_w1(0, 1)
-        w4_w = big([P, PASSES, N], I32, "w4_w", 1)
-        nc.sync.dma_start(w4_w[:], w4_words.rearrange("a p c i -> p a (c i)").bitcast(I32))
-        for t in range(PACK):
-            h[0, t] = features("h", 0, t)
-        quantise_w1(1, 0)
-        quantise_w1(1, 1)
-        tour.append(keep.tile([P, PACK, M], F32, name="tour1"))
-        w4_sc = w1_codes[0, 0][:, : N // 4].bitcast(U8)
-        for q in range(QUADS):
-            nc.sync.dma_start(
-                w1_codes[0, 0][32 * q : 32 * q + 8, : N // 4].bitcast(I32),
-                w4_scales[:, 4 * q : 4 * q + 4, :].bitcast(I32),
-            )
+        quantise_w1(0)
+        target_sb = big([P, N_TILES, M], F32, "target_sb", 2)
+        nc.sync.dma_start(target_sb[:], target.rearrange("(t p) m -> p t m", p=P))
+        tour.append(big([P, PACK, M], F32, "tour1", 0))
         for t in range(PACK):
             pick_tour(e[1, t], 1, t)
+        for t in range(PACK):
+            h[0, t] = features("h", 0, t)
+        docks0 = [keep.tile([P, M], F32, name=f"dock0{j}") for j in range(PACK)]
+        for j in range(PACK):
+            picked = h[0, j][:].indirect(pos_sb[DOCK][:])
+            if j < DOCKS_ON_VECTOR:
+                nc.vector.tensor_copy(docks0[j][:], picked)
+            else:
+                nc.scalar.activation(docks0[j][:], picked, ACT.Copy)
+        quantise_w1(1)
+        w4_w = ring.tile([P, PASSES, N], I32, name="w4_w", tag="w1_grouped", align_bytes=64)
+        nc.sync.dma_start(w4_w[:], w4_words.rearrange("a p c i -> p a (c i)").bitcast(I32))
+        w4_sc = w1_codes[0][:, 0, : N // 4].bitcast(U8)
+        for q in range(QUADS):
+            nc.sync.dma_start(
+                w1_codes[0][32 * q : 32 * q + 8, 0, : N // 4].bitcast(I32),
+                w4_scales[:, 4 * q : 4 * q + 4, :].bitcast(I32),
+            )
         h[1, 0] = features("h", 1, 0)
-        prod0 = keep.tile([P, PACK, M], F32, name="prod0")
+        addends = big([P, 2 * PACK, M], F32, "addends", 1)
+        prod0, lifts = addends[:, :PACK, :], addends[:, PACK:, :]
         z_t = keep.tile([P, M_TILES * PASS], BF16, name="z_t", align_bytes=64)
         for j in range(PACK):
             if j + 1 < PACK:
                 h[1, j + 1] = features("h", 1, j + 1)
             else:
-                first_docks = pick_docks(1, *PIECES[0])
-            dock = ring.tile([P, M], F32, name="dock0", bufs=4)
-            nc.vector.tensor_copy(dock[:], h[0, j][:].indirect(pos_sb[DOCK][:]))
+                early_docks = pick_docks(0, M // 2, on_vector=False)
+            dock = docks0[j]
             pick_product(prod0, 0, j, 0, M)
-            lift = ring.tile([P, M], F32, name="lift", bufs=4)
-            nc.vector.tensor_scalar(lift[:], dock[:], -2.0, 0.0, ALU.mult, ALU.max)
+            lift = lifts[:, j, :]
+            nc.vector.tensor_scalar(lift, dock[:], -2.0, 0.0, ALU.mult, ALU.max)
             turned = sums.tile([P, M_TILES, P], F32, name="acc")
             for mt in range(M_TILES):
                 cols = slice(mt * P, (mt + 1) * P)
@@ -272,8 +281,6 @@ def tile_list_cruise_slot_corrections_kernel(
                     )
             dst = z_t[:].rearrange("p (t u j q e) -> p t u j q e", u=2, j=PACK, q=32, e=2)[:, :, :, j, :, :]
             nc.scalar.copy(dst, turned[:].rearrange("p t (q u e) -> p t u q e", u=2, e=2))
-        target_sb = big([P, N_TILES, M], F32, "target_sb", 0)
-        nc.sync.dma_start(target_sb[:], target.rearrange("(t p) m -> p t m", p=P))
         grouped0 = keep.tile([P, M * PACK], BF16, name="z_grouped0", align_bytes=64)
         for pair in range(M_TILES // 2):
             back = sums.tile([P, 2, 2, P], F32, name="acc")
@@ -323,9 +330,11 @@ def tile_list_cruise_slot_corrections_kernel(
             nc.sync.dma_start(out.rearrange("(t p) m -> p t m", p=P)[:, first : first + count, lo:hi], sq[:])
 
         prod1 = pick_products(1, 0, M)
+        late_docks = pick_docks(M // 2, M, on_vector=True)
         banks, squared = [], []
         for lo, hi in PIECES:
-            z1 = quantise_z(first_docks if lo == 0 else pick_docks(1, lo, hi), prod1[:, :, lo:hi], 1, lo, hi)
+            docks = early_docks[:] if lo < M // 2 else late_docks[:, :, lo - M // 2 : hi - M // 2]
+            z1 = quantise_z(docks, prod1[:, :, lo:hi], 1, lo, hi)
             for job in squared:
                 finish(*job)
             squared = [residual(*job) for job in banks]

@@ -27,7 +27,9 @@ QUADS = 4
 LIST_COL = 16
 N_TILES = N // P
 M_TILES = M // P
-DOCKS_ON_VECTOR = 1
+TOURS_ON_VECTOR = 4
+LATE_ON_VECTOR = 4
+HOLD = 3
 PIECES = [(0, 256), (256, 384), (384, 512)]
 
 
@@ -115,8 +117,8 @@ def tile_list_cruise_slot_corrections_kernel(
             w2_raw[1][:].bitcast(U16).rearrange("p a (q t) -> p a t q", t=PACK),
         )
         w2_sc_by_pass = w2_sc_raw[:].rearrange("p (a c) -> p a c", a=PASSES)
-        dealt_sc = keep.tile([P, PASSES, PASS], U8, name="w2_sc_dealt", align_bytes=64)
-        nc.gpsimd.tensor_copy(
+        dealt_sc = keep.tile([P, PASSES, PASS], U8, name="w2_sc_dealt", tag="w2_raw1", align_bytes=64)
+        nc.vector.tensor_copy(
             dealt_sc[:].rearrange("p a (t q) -> p a t q", t=PACK),
             w2_sc_by_pass[:, :, PASS:].rearrange("p a (q t) -> p a t q", t=PACK),
         )
@@ -130,19 +132,19 @@ def tile_list_cruise_slot_corrections_kernel(
 
         def group_w1(b, a, grouped):
             raw = w1_raw[b, a]
+            if b == 1:
+                nc.vector.tensor_copy(
+                    grouped.rearrange("p (u e q) j -> p u q j e", u=2, e=2),
+                    raw.rearrange("p j (q u e) -> p u q j e", u=2, e=2),
+                )
+                return
             for piece in range(4):
-                if b == 0:
-                    cols = slice(piece * P, (piece + 1) * P)
-                    dst = grouped[:, cols, :].rearrange("p (c i) j -> p c j i", i=4)
-                    src = raw[:, :, cols].rearrange("p j (c i) -> p c j i", i=4)
-                else:
-                    u, rows = piece // 2, slice(piece % 2 * (P // 2), (piece % 2 + 1) * (P // 2))
-                    dst = grouped.rearrange("p (u e q) j -> p u q j e", u=2, e=2)[:, u, rows]
-                    src = raw.rearrange("p j (q u e) -> p u q j e", u=2, e=2)[:, u, rows]
+                dst = grouped[:, piece * P : (piece + 1) * P, :]
+                src = raw[:, :, piece * P : (piece + 1) * P].rearrange("p j c -> p c j")
                 nc.gpsimd.tensor_scalar(dst, src, 1.0, 0.0, ALU.mult, ALU.add)
 
         def quantise_w1(b):
-            grouped = ring.tile([P, PASSES * PASS, PACK], BF16, name="w1_grouped", tag="w1_grouped", align_bytes=64)
+            grouped = ring.tile([P, PASSES * PASS, PACK], BF16, name="w1_grouped", tag="w1_grouped", bufs=1, align_bytes=64)
             for a in range(PASSES):
                 group_w1(b, a, grouped[:, a * PASS : (a + 1) * PASS, :])
             codes = keep.tile([P, PASSES, PASS], U32, name=f"w1_codes{b}", align_bytes=64)
@@ -188,29 +190,26 @@ def tile_list_cruise_slot_corrections_kernel(
 
 
         def pick_tour(window, b, t):
-            nc.vector.tensor_copy(tour[b][:, t, :], window[:].indirect(pos_sb[TOUR][:]))
+            picked = window[:].indirect(pos_sb[TOUR][:])
+            if b * PACK + t < TOURS_ON_VECTOR:
+                nc.vector.tensor_copy(tour[b][:, t, :], picked)
+            else:
+                nc.scalar.activation(tour[b][:, t, :], picked, ACT.Copy)
 
-        def pick_product(prod, b, t, lo, hi):
-            nc.vector.tensor_tensor(
-                prod[:, t, :], h[b, t][:].indirect(places(SAIL, lo, hi)), tour[b][:, t, lo:hi], ALU.mult
-            )
-
-        def pick_products(b, lo, hi):
-            prod = keep.tile([P, PACK, hi - lo], F32, name=f"prod{b}_{lo}")
-            for t in range(PACK):
-                pick_product(prod, b, t, lo, hi)
-            return prod
+        def pick_product(prod, b, t):
+            nc.vector.tensor_tensor(prod, h[b, t][:].indirect(pos_sb[SAIL][:]), tour[b][:, t, :], ALU.mult)
 
         def pick_docks(lo, hi, on_vector):
-            dock = keep.tile([P, PACK, hi - lo], F32, name=f"dock1_{lo}")
+            dock = keep.tile([P, PACK, hi - lo], F32, name=f"dock1_{lo}", tag="late" if lo else f"prod0{HOLD}")
             for t in range(PACK):
                 picked = h[1, t][:].indirect(places(DOCK, lo, hi))
-                if on_vector:
+                if t < on_vector:
                     nc.vector.tensor_copy(dock[:, t, :], picked)
                 else:
                     nc.scalar.activation(dock[:, t, :], picked, ACT.Copy)
-            nc.scalar.activation(dock[:], dock[:], ACT.Abs)
-            return dock
+            size = keep.tile([P, PACK, hi - lo], F32, name=f"size{lo}", tag="z_t" if lo else "size", align_bytes=64)
+            nc.scalar.activation(size[:], dock[:], ACT.Abs)
+            return size
 
         def quantise(grouped, name):
             width = grouped.shape[1] // PACK
@@ -237,20 +236,13 @@ def tile_list_cruise_slot_corrections_kernel(
         quantise_w1(0)
         target_sb = big([P, N_TILES, M], F32, "target_sb", 2)
         nc.sync.dma_start(target_sb[:], target.rearrange("(t p) m -> p t m", p=P))
-        tour.append(big([P, PACK, M], F32, "tour1", 0))
-        for t in range(PACK):
-            pick_tour(e[1, t], 1, t)
+        quantise_w1(1)
+        tour.append(big([P, PACK, M], F32, "tour1", 1))
         for t in range(PACK):
             h[0, t] = features("h", 0, t)
-        docks0 = [keep.tile([P, M], F32, name=f"dock0{j}") for j in range(PACK)]
-        for j in range(PACK):
-            picked = h[0, j][:].indirect(pos_sb[DOCK][:])
-            if j < DOCKS_ON_VECTOR:
-                nc.vector.tensor_copy(docks0[j][:], picked)
-            else:
-                nc.scalar.activation(docks0[j][:], picked, ACT.Copy)
-        quantise_w1(1)
-        w4_w = ring.tile([P, PASSES, N], I32, name="w4_w", tag="w1_grouped", align_bytes=64)
+        for t in range(PACK):
+            pick_tour(e[1, t], 1, t)
+        w4_w = ring.tile([P, PASSES, N], I32, name="w4_w", tag="w1_grouped", bufs=1, align_bytes=64)
         nc.sync.dma_start(w4_w[:], w4_words.rearrange("a p c i -> p a (c i)").bitcast(I32))
         w4_sc = w1_codes[0][:, 0, : N // 4].bitcast(U8)
         for q in range(QUADS):
@@ -259,28 +251,27 @@ def tile_list_cruise_slot_corrections_kernel(
                 w4_scales[:, 4 * q : 4 * q + 4, :].bitcast(I32),
             )
         h[1, 0] = features("h", 1, 0)
-        addends = big([P, 2 * PACK, M], F32, "addends", 1)
-        prod0, lifts = addends[:, :PACK, :], addends[:, PACK:, :]
-        z_t = keep.tile([P, M_TILES * PASS], BF16, name="z_t", align_bytes=64)
+        z_t = keep.tile([P, M_TILES * PASS], BF16, name="z_t", tag="z_t", align_bytes=64)
         for j in range(PACK):
             if j + 1 < PACK:
                 h[1, j + 1] = features("h", 1, j + 1)
-            else:
-                early_docks = pick_docks(0, M // 2, on_vector=False)
-            dock = docks0[j]
-            pick_product(prod0, 0, j, 0, M)
-            lift = lifts[:, j, :]
-            nc.vector.tensor_scalar(lift, dock[:], -2.0, 0.0, ALU.mult, ALU.max)
+            dock = keep.tile([P, M], F32, name=f"dock0{j}")
+            nc.vector.tensor_copy(dock[:], h[0, j][:].indirect(pos_sb[DOCK][:]))
+            prod = keep.tile([P, M], F32, name=f"prod0{j}", tag=f"prod0{j}")
+            pick_product(prod[:], 0, j)
+            lift = keep.tile([P, M], F32, name=f"lift{j}")
+            nc.vector.tensor_scalar(lift[:], dock[:], -2.0, 0.0, ALU.mult, ALU.max)
             turned = sums.tile([P, M_TILES, P], F32, name="acc")
             for mt in range(M_TILES):
                 cols = slice(mt * P, (mt + 1) * P)
-                terms = (dock[:, cols], lift[:, cols], prod0[:, j, cols])
+                terms = (dock[:, cols], lift[:, cols], prod[:, cols])
                 for i, term in enumerate(terms):
                     nc.tensor.matmul(
                         turned[:, mt, :], term, ident[:], start=(i == 0), stop=(i == 2), is_transpose=True
                     )
             dst = z_t[:].rearrange("p (t u j q e) -> p t u j q e", u=2, j=PACK, q=32, e=2)[:, :, :, j, :, :]
             nc.scalar.copy(dst, turned[:].rearrange("p t (q u e) -> p t u q e", u=2, e=2))
+        early_docks = pick_docks(0, M // 2, on_vector=0)
         grouped0 = keep.tile([P, M * PACK], BF16, name="z_grouped0", align_bytes=64)
         for pair in range(M_TILES // 2):
             back = sums.tile([P, 2, 2, P], F32, name="acc")
@@ -329,8 +320,10 @@ def tile_list_cruise_slot_corrections_kernel(
             nc.vector.tensor_tensor(sq[:], sq[:], res[:], ALU.mult)
             nc.sync.dma_start(out.rearrange("(t p) m -> p t m", p=P)[:, first : first + count, lo:hi], sq[:])
 
-        prod1 = pick_products(1, 0, M)
-        late_docks = pick_docks(M // 2, M, on_vector=True)
+        prod1 = keep.tile([P, PACK, M], F32, name="prod1")
+        for t in range(PACK):
+            pick_product(prod1[:, t, :], 1, t)
+        late_docks = pick_docks(M // 2, M, on_vector=LATE_ON_VECTOR)
         banks, squared = [], []
         for lo, hi in PIECES:
             docks = early_docks[:] if lo < M // 2 else late_docks[:, :, lo - M // 2 : hi - M // 2]

@@ -138,6 +138,11 @@ def tile_list_cruise_slot_corrections_kernel(
                     raw.rearrange("p j (q u e) -> p u q j e", u=2, e=2),
                 )
                 return
+            if a == 1:
+                nc.vector.tensor_copy(
+                    grouped.rearrange("p (c i) j -> p c j i", i=4), raw.rearrange("p j (c i) -> p c j i", i=4)
+                )
+                return
             for piece in range(4):
                 dst = grouped[:, piece * P : (piece + 1) * P, :]
                 src = raw[:, :, piece * P : (piece + 1) * P].rearrange("p j c -> p c j")

@@ -50,7 +50,7 @@ def tile_list_cruise_slot_corrections_kernel(
         pos_sb = [keep.tile([P, M // LIST_COL], U16, name=f"pos{i + 1}_sb") for i in range(3)]
         DOCK, TOUR, SAIL = 0, 1, 2
 
-        tab_sc = big([P, T], U8, "tab_sc", 2)
+        tab_sc = keep.tile([P, T], U8, name="tab_sc", align_bytes=64)
         nc.vector.memset(tab_sc[:].bitcast(I32), 0)
         w2_sc_raw = keep.tile([P, PASSES * H], U8, name="w2_sc_raw", align_bytes=64)
         nc.gpsimd.memset(w2_sc_raw[:].bitcast(I32), 0)
@@ -96,7 +96,6 @@ def tile_list_cruise_slot_corrections_kernel(
             nc.scalar.dma_start(
                 v_sc1[32 * q : 32 * q + 4, :].bitcast(I32), v_sc[32 * q + 4 : 32 * q + 8, :].bitcast(I32)
             )
-        load_w1(0, 0, big([P, PACK, PASS], F32, "w1_raw00", 2)[:])
         v_w = {}
 
         def gather_words(a, pieces):
@@ -108,7 +107,9 @@ def tile_list_cruise_slot_corrections_kernel(
             v_w[a] = words
 
         gather_words(0, 1)
-        load_w1(0, 1, big([P, PACK, PASS], F32, "w1_raw01", 0)[:])
+        w1_first = big([P, PASSES * PACK, PASS], F32, "w1_raw0", 0)
+        for a in range(PASSES):
+            load_w1(0, a, w1_first[:, a * PACK : (a + 1) * PACK, :])
         gather_words(1, HALVES)
 
         dealt_w = keep.tile([P, PASSES, 2 * PASS], U8, name="w2_dealt", align_bytes=64)
@@ -226,9 +227,9 @@ def tile_list_cruise_slot_corrections_kernel(
         def quantise_z(dock, prod, b, lo, hi):
             grouped = keep.tile([P, hi - lo, PACK], BF16, name=f"z_grouped{b}_{lo}", align_bytes=64)
             nc.vector.tensor_tensor(
-                grouped[:].rearrange("p (c i) t -> p c t i", i=4),
-                dock.rearrange("p t (c i) -> p c t i", i=4),
-                prod.rearrange("p t (c i) -> p c t i", i=4),
+                grouped[:].rearrange("p (c i) t -> p c t i", i=2),
+                dock.rearrange("p t (c i) -> p c t i", i=2),
+                prod.rearrange("p t (c i) -> p c t i", i=2),
                 ALU.add,
             )
             return quantise(grouped[:].rearrange("p m t -> p (m t)"), f"z{b}_{lo}")
@@ -239,7 +240,7 @@ def tile_list_cruise_slot_corrections_kernel(
         for t in range(PACK):
             pick_tour(e[0, t], 0, t)
         quantise_w1(0)
-        target_sb = big([P, N_TILES, M], F32, "target_sb", 2)
+        target_sb = big([P, N_TILES, M], F32, "target_sb", 0)
         nc.sync.dma_start(target_sb[:], target.rearrange("(t p) m -> p t m", p=P))
         quantise_w1(1)
         tour.append(big([P, PACK, M], F32, "tour1", 1))

@@ -51,9 +51,9 @@ def tile_list_cruise_slot_corrections_kernel(
         DOCK, TOUR, SAIL = 0, 1, 2
 
         tab_sc = keep.tile([P, T], U8, name="tab_sc", align_bytes=64)
-        nc.vector.memset(tab_sc[:].bitcast(I32), 0)
+        nc.gpsimd.memset(tab_sc[:].bitcast(I32), 0)
         w2_sc_raw = keep.tile([P, PASSES * H], U8, name="w2_sc_raw", align_bytes=64)
-        nc.gpsimd.memset(w2_sc_raw[:].bitcast(I32), 0)
+        nc.vector.memset(w2_sc_raw[:].bitcast(I32), 0)
         for q in range(QUADS):
             nc.gpsimd.dma_start(
                 w2_sc_raw[32 * q : 32 * q + 4, :].bitcast(I32).rearrange("r (a c) -> r a c", a=PASSES),
@@ -323,7 +323,8 @@ def tile_list_cruise_slot_corrections_kernel(
             return res, sq, first, count, lo, hi
 
         def finish(res, sq, first, count, lo, hi):
-            nc.vector.tensor_tensor(sq[:], sq[:], res[:], ALU.mult)
+            engine = nc.gpsimd if (lo, first) == (0, 0) else nc.vector
+            engine.tensor_tensor(sq[:], sq[:], res[:], ALU.mult)
             nc.sync.dma_start(out.rearrange("(t p) m -> p t m", p=P)[:, first : first + count, lo:hi], sq[:])
 
         prod1 = keep.tile([P, PACK, M], F32, name="prod1")

@@ -39,19 +39,26 @@ def tile_list_cruise_slot_corrections_kernel(
     nc = tc.nc
     with ExitStack() as ctx:
         keep = ctx.enter_context(tc.tile_pool(name="keep", bufs=1))
+        placed = ctx.enter_context(tc.tile_pool(name="placed", bufs=1))
         ring = ctx.enter_context(tc.tile_pool(name="ring", bufs=2))
         e_windows = ctx.enter_context(tc.tile_pool(name="e_windows", bufs=8))
         sums = ctx.enter_context(tc.psum_pool(name="sums", bufs=8))
 
+        def at(kib, shape, dtype, name):
+            return placed.tile(shape, dtype, name=name, offset=kib * 1024, align_bytes=64)
+
         def big(shape, dtype, name, buffer):
-            return keep.tile(shape, dtype, name=name, tag=f"big{buffer}", align_bytes=64)
+            if name == "tab_w0":
+                return at(0, shape, dtype, name)
+            return at(2 + 16 * buffer, shape, dtype, name)
 
         offs_sb = keep.tile([P, S // LIST_COL], U16, name="offs_sb")
         pos_sb = [keep.tile([P, M // LIST_COL], U16, name=f"pos{i + 1}_sb") for i in range(3)]
         DOCK, TOUR, SAIL = 0, 1, 2
 
         tab_sc = keep.tile([P, T], U8, name="tab_sc", align_bytes=64)
-        nc.gpsimd.memset(tab_sc[:].bitcast(I32), 0)
+        nc.gpsimd.memset(tab_sc[64:, :].bitcast(I32), 0)
+        nc.gpsimd.memset(tab_sc[32:64, :].bitcast(I32), 0)
         w2_sc_raw = keep.tile([P, PASSES * H], U8, name="w2_sc_raw", align_bytes=64)
         nc.vector.memset(w2_sc_raw[:].bitcast(I32), 0)
         for q in range(QUADS):
@@ -59,13 +66,12 @@ def tile_list_cruise_slot_corrections_kernel(
                 w2_sc_raw[32 * q : 32 * q + 4, :].bitcast(I32).rearrange("r (a c) -> r a c", a=PASSES),
                 w2_scales[:, 4 * q : 4 * q + 4, :].rearrange("a r c -> r a c").bitcast(I32),
             )
-        v_sc1 = keep.tile([P, S], U8, name="v_sc1", align_bytes=64)
-        nc.vector.memset(v_sc1[:].bitcast(I32), 0)
+        planes = keep.tile([P, PASSES * S], U8, name="planes", align_bytes=64)
+        nc.vector.memset(planes[:].bitcast(I32), 0)
 
         tab_w = [big([P, T], I32, f"tab_w{a}", a) for a in range(PASSES)]
         ident = keep.tile([P, P], F32, name="ident")
-        make_identity(nc, ident[:])
-        w2_raw = [keep.tile([P, PASSES, 2 * PASS], U8, name=f"w2_raw{b}", tag=f"w2_raw{b}", align_bytes=64) for b in range(PASSES)]
+        w2_raw = [keep.tile([P, PASSES, 2 * PASS], U8, name="w2_raw0", align_bytes=64)]
         w1_raw = {}
 
         def load_table_words(a):
@@ -77,25 +83,23 @@ def tile_list_cruise_slot_corrections_kernel(
             w1_raw[b, a] = raw
 
         nc.sync.dma_start(offs_sb[:], offs)
+        nc.sync.dma_start(tab_sc[:32, :].bitcast(I32), tab_scales.rearrange("a r t -> (a r) t").bitcast(I32))
+        w2_halves = w2_words.rearrange("a p (b c) -> b p a c", b=PASSES)
+        nc.sync.dma_start(w2_raw[0][:].bitcast(I32), w2_halves[0].bitcast(I32))
         nc.sync.dma_start(pos_sb[TOUR][:], pos2)
         nc.sync.dma_start(pos_sb[SAIL][:], pos3)
-        for q in range(QUADS):
-            nc.sync.dma_start(
-                tab_sc[32 * q : 32 * q + 8, :].bitcast(I32), tab_scales[:, 4 * q : 4 * q + 4, :].bitcast(I32)
-            )
+        nc.sync.dma_start(pos_sb[DOCK][:], pos1)
         load_table_words(0)
         load_table_words(1)
-        w2_halves = w2_words.rearrange("a p (b c) -> b p a c", b=PASSES)
-        for b in range(PASSES):
-            nc.sync.dma_start(w2_raw[b][:].bitcast(I32), w2_halves[b].bitcast(I32))
-        nc.sync.dma_start(pos_sb[DOCK][:], pos1)
 
         v_sc = keep.tile([P, S], U8, name="v_sc", align_bytes=64)
         nc.vector.tensor_copy(v_sc[:], tab_sc[:].indirect(offs_sb[:]))
-        for q in range(QUADS):
-            nc.scalar.dma_start(
-                v_sc1[32 * q : 32 * q + 4, :].bitcast(I32), v_sc[32 * q + 4 : 32 * q + 8, :].bitcast(I32)
-            )
+        for a in range(PASSES):
+            for q in range(QUADS):
+                row = 16 * a + 4 * q
+                move = nc.scalar.dma_start if row else nc.vector.tensor_copy
+                move(planes[32 * q : 32 * q + 4, a * S : (a + 1) * S].bitcast(I32), v_sc[row : row + 4, :].bitcast(I32))
+        make_identity(nc, ident[:])
         v_w = {}
 
         def gather_words(a, pieces):
@@ -107,6 +111,8 @@ def tile_list_cruise_slot_corrections_kernel(
             v_w[a] = words
 
         gather_words(0, 1)
+        w2_raw.append(at(0, [P, PASSES, 2 * PASS], U8, "w2_raw1"))
+        nc.sync.dma_start(w2_raw[1][:].bitcast(I32), w2_halves[1].bitcast(I32))
         w1_first = big([P, PASSES * PACK, PASS], F32, "w1_raw0", 0)
         for a in range(PASSES):
             load_w1(0, a, w1_first[:, a * PACK : (a + 1) * PACK, :])
@@ -118,7 +124,7 @@ def tile_list_cruise_slot_corrections_kernel(
             w2_raw[1][:].bitcast(U16).rearrange("p a (q t) -> p a t q", t=PACK),
         )
         w2_sc_by_pass = w2_sc_raw[:].rearrange("p (a c) -> p a c", a=PASSES)
-        dealt_sc = keep.tile([P, PASSES, PASS], U8, name="w2_sc_dealt", tag="w2_raw1", align_bytes=64)
+        dealt_sc = at(0, [P, PASSES, PASS], U8, "w2_sc_dealt")
         nc.vector.tensor_copy(
             dealt_sc[:].rearrange("p a (t q) -> p a t q", t=PACK),
             w2_sc_by_pass[:, :, PASS:].rearrange("p a (q t) -> p a t q", t=PACK),
@@ -174,17 +180,15 @@ def tile_list_cruise_slot_corrections_kernel(
                     if kind == "h":
                         weights = w1_codes[b][:, a, t * P : (t + 1) * P].bitcast(E4M3)
                         weight_sc = w1_sc[b][:, a, t * P : (t + 1) * P]
-                        moving_sc = v_sc[4 * a :, cols]
                     else:
                         weights = w2_w[b][:, a, 2 * t * P : 2 * (t + 1) * P].bitcast(E2M1)
                         weight_sc = w2_sc[b][:, a, t * P : (t + 1) * P]
-                        moving_sc = (v_sc, v_sc1)[a][:, cols]
                     nc.tensor.matmul_mx(
                         out=acc[:],
                         lhsT=weights,
                         lhsT_scale=weight_sc,
                         rhs=v_w[a][:, cols].bitcast(E4M3),
-                        rhs_scale=moving_sc,
+                        rhs_scale=planes[:, a * S + half * BANK : a * S + (half + 1) * BANK],
                         start=(a == 0),
                         stop=(a == PASSES - 1),
                     )

@@ -176,7 +176,8 @@ def tile_list_cruise_slot_corrections_kernel(
             for half in range(HALVES):
                 cols = slice(half * BANK, (half + 1) * BANK)
                 acc = sums.tile([P, BANK], F32, name="acc")
-                for a in range(PASSES):
+                order = (0, 1) if (kind, b, t) == ("e", 0, 0) else (1, 0)
+                for i, a in enumerate(order):
                     if kind == "h":
                         weights = w1_codes[b][:, a, t * P : (t + 1) * P].bitcast(E4M3)
                         weight_sc = w1_sc[b][:, a, t * P : (t + 1) * P]
@@ -189,8 +190,8 @@ def tile_list_cruise_slot_corrections_kernel(
                         lhsT_scale=weight_sc,
                         rhs=v_w[a][:, cols].bitcast(E4M3),
                         rhs_scale=planes[:, a * S + half * BANK : a * S + (half + 1) * BANK],
-                        start=(a == 0),
-                        stop=(a == PASSES - 1),
+                        start=(i == 0),
+                        stop=(i == PASSES - 1),
                     )
                 nc.scalar.copy(window[:, cols], acc[:])
             return window

@@ -30,7 +30,7 @@ M_TILES = M // P
 TOURS_ON_VECTOR = 4
 LATE_ON_VECTOR = 4
 HOLD = 3
-PIECES = [(0, 256), (256, 384), (384, 512)]
+PIECES = [(0, 256), (256, 512)]
 
 
 def tile_list_cruise_slot_corrections_kernel(
@@ -85,19 +85,20 @@ def tile_list_cruise_slot_corrections_kernel(
         nc.sync.dma_start(offs_sb[:], offs)
         nc.sync.dma_start(tab_sc[:32, :].bitcast(I32), tab_scales.rearrange("a r t -> (a r) t").bitcast(I32))
         w2_halves = w2_words.rearrange("a p (b c) -> b p a c", b=PASSES)
-        nc.sync.dma_start(w2_raw[0][:].bitcast(I32), w2_halves[0].bitcast(I32))
+        load_table_words(0)
         nc.sync.dma_start(pos_sb[TOUR][:], pos2)
         nc.sync.dma_start(pos_sb[SAIL][:], pos3)
         nc.sync.dma_start(pos_sb[DOCK][:], pos1)
-        load_table_words(0)
         load_table_words(1)
+        nc.sync.dma_start(w2_raw[0][:].bitcast(I32), w2_halves[0].bitcast(I32))
 
         v_sc = keep.tile([P, S], U8, name="v_sc", align_bytes=64)
         nc.vector.tensor_copy(v_sc[:], tab_sc[:].indirect(offs_sb[:]))
         for a in range(PASSES):
             for q in range(QUADS):
                 row = 16 * a + 4 * q
-                move = nc.scalar.dma_start if row else nc.vector.tensor_copy
+                queue = (nc.scalar, nc.sync)[a]
+                move = queue.dma_start if row else nc.vector.tensor_copy
                 move(planes[32 * q : 32 * q + 4, a * S : (a + 1) * S].bitcast(I32), v_sc[row : row + 4, :].bitcast(I32))
         make_identity(nc, ident[:])
         v_w = {}
@@ -321,8 +322,8 @@ def tile_list_cruise_slot_corrections_kernel(
             return banks
 
         def residual(y, first, count, lo, hi):
-            res = ring.tile([P, count, hi - lo], F32, name="res", bufs=5)
-            sq = ring.tile([P, count, hi - lo], F32, name="sq", bufs=5)
+            res = ring.tile([P, count, hi - lo], F32, name="res", bufs=6)
+            sq = ring.tile([P, count, hi - lo], F32, name="sq", bufs=6)
             nc.vector.tensor_tensor(res[:], target_sb[:, first : first + count, lo:hi], y, ALU.subtract)
             nc.scalar.activation(sq[:], res[:], ACT.Square)
             return res, sq, first, count, lo, hi
@@ -344,8 +345,8 @@ def tile_list_cruise_slot_corrections_kernel(
                 finish(*job)
             squared = [residual(*job) for job in banks]
             banks = [(y[:], first, count, lo, hi) for y, first, count in scores(lo, hi, z1)]
-        y, first, count, lo, hi = banks[0]
-        half = count // 2
-        last = [residual(y[:, i * half : (i + 1) * half, :], i * half, half, lo, hi) for i in range(2)]
-        for job in squared + last:
+        for job in squared:
+            finish(*job)
+        last = [residual(y[:, i : i + 1, :], first + i, 1, lo, hi) for y, first, count, lo, hi in banks for i in range(count)]
+        for job in last:
             finish(*job)

from contextlib import ExitStack

import concourse.mybir as mybir
from concourse.masks import make_identity

K, H, N, T, S, M = 1024, 1024, 512, 2048, 1024, 512
FLOPS = 2 * K * H * S * 2 + 2 * H * N * M

F32 = mybir.dt.float32
BF16 = mybir.dt.bfloat16
I32 = mybir.dt.int32
U32 = mybir.dt.uint32
U16 = mybir.dt.uint16
U8 = mybir.dt.uint8
E4M3 = mybir.dt.float8_e4m3fn_x4
E2M1 = mybir.dt.float4_e2m1fn_x4
ACT = mybir.ActivationFunctionType
ALU = mybir.AluOpType

P = 128
PACK = 4
PASS = P * PACK
PASSES = 2
BANK = 512
HALVES = S // BANK
QUADS = 4
LIST_COL = 16
N_TILES = N // P
M_TILES = M // P
TOURS_ON_VECTOR = 4
LATE_ON_VECTOR = 4
HOLD = 3
PIECES = [(0, 256), (256, 512)]


def tile_list_cruise_slot_corrections_kernel(
    tc, tab_words, tab_scales, offs, pos1, pos2, pos3, w1, w2_words, w2_scales, w4_words, w4_scales, target, out
):
    nc = tc.nc
    with ExitStack() as ctx:
        keep = ctx.enter_context(tc.tile_pool(name="keep", bufs=1))
        placed = ctx.enter_context(tc.tile_pool(name="placed", bufs=1))
        ring = ctx.enter_context(tc.tile_pool(name="ring", bufs=2))
        e_windows = ctx.enter_context(tc.tile_pool(name="e_windows", bufs=8))
        sums = ctx.enter_context(tc.psum_pool(name="sums", bufs=8))

        def at(kib, shape, dtype, name):
            return placed.tile(shape, dtype, name=name, offset=kib * 1024, align_bytes=64)

        def big(shape, dtype, name, buffer):
            if name == "tab_w0":
                return at(0, shape, dtype, name)
            return at(2 + 16 * buffer, shape, dtype, name)

        offs_sb = keep.tile([P, S // LIST_COL], U16, name="offs_sb")
        pos_sb = [keep.tile([P, M // LIST_COL], U16, name=f"pos{i + 1}_sb") for i in range(3)]
        DOCK, TOUR, SAIL = 0, 1, 2

        tab_sc = keep.tile([P, T], U8, name="tab_sc", align_bytes=64)
        nc.gpsimd.memset(tab_sc[64:, :].bitcast(I32), 0)
        nc.gpsimd.memset(tab_sc[32:64, :].bitcast(I32), 0)
        w2_sc_raw = keep.tile([P, PASSES * H], U8, name="w2_sc_raw", align_bytes=64)
        nc.vector.memset(w2_sc_raw[:].bitcast(I32), 0)
        for q in range(QUADS):
            nc.gpsimd.dma_start(
                w2_sc_raw[32 * q : 32 * q + 4, :].bitcast(I32).rearrange("r (a c) -> r a c", a=PASSES),
                w2_scales[:, 4 * q : 4 * q + 4, :].rearrange("a r c -> r a c").bitcast(I32),
            )
        planes = keep.tile([P, PASSES * S], U8, name="planes", align_bytes=64)
        nc.vector.memset(planes[:].bitcast(I32), 0)

        tab_w = [big([P, T], I32, f"tab_w{a}", a) for a in range(PASSES)]
        ident = keep.tile([P, P], F32, name="ident")
        w2_raw = [keep.tile([P, PASSES, 2 * PASS], U8, name="w2_raw0", align_bytes=64)]
        w1_raw = {}

        def load_table_words(a):
            nc.sync.dma_start(tab_w[a][:], tab_words[a].rearrange("p t i -> p (t i)").bitcast(I32))

        def load_w1(b, a, raw):
            rows = w1[a * PASS : (a + 1) * PASS, b * PASS : (b + 1) * PASS]
            nc.sync.dma_start(raw, rows.rearrange("(p j) c -> p j c", j=PACK))
            w1_raw[b, a] = raw

        nc.sync.dma_start(offs_sb[:], offs)
        nc.sync.dma_start(tab_sc[:32, :].bitcast(I32), tab_scales.rearrange("a r t -> (a r) t").bitcast(I32))
        w2_halves = w2_words.rearrange("a p (b c) -> b p a c", b=PASSES)
        load_table_words(0)
        nc.sync.dma_start(pos_sb[TOUR][:], pos2)
        nc.sync.dma_start(pos_sb[SAIL][:], pos3)
        nc.sync.dma_start(pos_sb[DOCK][:], pos1)
        load_table_words(1)
        nc.sync.dma_start(w2_raw[0][:].bitcast(I32), w2_halves[0].bitcast(I32))

        v_sc = keep.tile([P, S], U8, name="v_sc", align_bytes=64)
        nc.vector.tensor_copy(v_sc[:], tab_sc[:].indirect(offs_sb[:]))
        for a in range(PASSES):
            for q in range(QUADS):
                row = 16 * a + 4 * q
                queue = (nc.scalar, nc.sync)[a]
                move = queue.dma_start if row else nc.vector.tensor_copy
                move(planes[32 * q : 32 * q + 4, a * S : (a + 1) * S].bitcast(I32), v_sc[row : row + 4, :].bitcast(I32))
        make_identity(nc, ident[:])
        v_w = {}

        def gather_words(a, pieces):
            words = keep.tile([P, S], U32, name=f"v_w{a}", align_bytes=64)
            step = S // pieces
            for lo in range(0, S, step):
                entries = offs_sb[:, lo // LIST_COL : (lo + step) // LIST_COL]
                nc.vector.tensor_copy(words[:, lo : lo + step], tab_w[a][:].bitcast(U32).indirect(entries))
            v_w[a] = words

        gather_words(0, 1)
        w2_raw.append(at(0, [P, PASSES, 2 * PASS], U8, "w2_raw1"))
        nc.sync.dma_start(w2_raw[1][:].bitcast(I32), w2_halves[1].bitcast(I32))
        w1_first = big([P, PASSES * PACK, PASS], F32, "w1_raw0", 0)
        for a in range(PASSES):
            load_w1(0, a, w1_first[:, a * PACK : (a + 1) * PACK, :])
        gather_words(1, HALVES)

        dealt_w = keep.tile([P, PASSES, 2 * PASS], U8, name="w2_dealt", align_bytes=64)
        nc.vector.tensor_copy(
            dealt_w[:].bitcast(U16).rearrange("p a (t q) -> p a t q", t=PACK),
            w2_raw[1][:].bitcast(U16).rearrange("p a (q t) -> p a t q", t=PACK),
        )
        w2_sc_by_pass = w2_sc_raw[:].rearrange("p (a c) -> p a c", a=PASSES)
        dealt_sc = at(0, [P, PASSES, PASS], U8, "w2_sc_dealt")
        nc.vector.tensor_copy(
            dealt_sc[:].rearrange("p a (t q) -> p a t q", t=PACK),
            w2_sc_by_pass[:, :, PASS:].rearrange("p a (q t) -> p a t q", t=PACK),
        )
        w2_w = [w2_raw[0], dealt_w]
        w2_sc = [w2_sc_by_pass, dealt_sc]
        w1_second = big([P, PASSES * PACK, PASS], F32, "w1_raw1", 1)
        for a in range(PASSES):
            load_w1(1, a, w1_second[:, a * PACK : (a + 1) * PACK, :])

        w1_codes, w1_sc = {}, {}

        def group_w1(b, a, grouped):
            raw = w1_raw[b, a]
            if b == 1:
                nc.vector.tensor_copy(
                    grouped.rearrange("p (u e q) j -> p u q j e", u=2, e=2),
                    raw.rearrange("p j (q u e) -> p u q j e", u=2, e=2),
                )
                return
            if a == 1:
                nc.vector.tensor_copy(
                    grouped.rearrange("p (c i) j -> p c j i", i=4), raw.rearrange("p j (c i) -> p c j i", i=4)
                )
                return
            for piece in range(4):
                dst = grouped[:, piece * P : (piece + 1) * P, :]
                src = raw[:, :, piece * P : (piece + 1) * P].rearrange("p j c -> p c j")
                nc.gpsimd.tensor_scalar(dst, src, 1.0, 0.0, ALU.mult, ALU.add)

        def quantise_w1(b):
            grouped = ring.tile([P, PASSES * PASS, PACK], BF16, name="w1_grouped", tag="w1_grouped", bufs=1, align_bytes=64)
            for a in range(PASSES):
                group_w1(b, a, grouped[:, a * PASS : (a + 1) * PASS, :])
            codes = keep.tile([P, PASSES, PASS], U32, name=f"w1_codes{b}", align_bytes=64)
            scales = keep.tile([P, PASSES, PASS], U8, name=f"w1_sc{b}", align_bytes=64)
            nc.vector.quantize_mx(
                out=codes[:].rearrange("p a c -> p (a c)").bitcast(E4M3),
                scales=scales[:].rearrange("p a c -> p (a c)"),
                in_=grouped[:].rearrange("p c j -> p (c j)"),
            )
            w1_codes[b], w1_sc[b] = codes, scales

        def features(kind, b, t):
            if kind == "h":
                window = keep.tile([P, S], F32, name=f"h{b}{t}")
            else:
                window = e_windows.tile([P, S], F32, name="e")
            for half in range(HALVES):
                cols = slice(half * BANK, (half + 1) * BANK)
                acc = sums.tile([P, BANK], F32, name="acc")
                order = (0, 1) if (kind, b, t) == ("e", 0, 0) else (1, 0)
                for i, a in enumerate(order):
                    if kind == "h":
                        weights = w1_codes[b][:, a, t * P : (t + 1) * P].bitcast(E4M3)
                        weight_sc = w1_sc[b][:, a, t * P : (t + 1) * P]
                    else:
                        weights = w2_w[b][:, a, 2 * t * P : 2 * (t + 1) * P].bitcast(E2M1)
                        weight_sc = w2_sc[b][:, a, t * P : (t + 1) * P]
                    nc.tensor.matmul_mx(
                        out=acc[:],
                        lhsT=weights,
                        lhsT_scale=weight_sc,
                        rhs=v_w[a][:, cols].bitcast(E4M3),
                        rhs_scale=planes[:, a * S + half * BANK : a * S + (half + 1) * BANK],
                        start=(i == 0),
                        stop=(i == PASSES - 1),
                    )
                nc.scalar.copy(window[:, cols], acc[:])
            return window

        def places(which, lo, hi):
            return pos_sb[which][:, lo // LIST_COL : hi // LIST_COL]


        def pick_tour(window, b, t):
            picked = window[:].indirect(pos_sb[TOUR][:])
            if b * PACK + t < TOURS_ON_VECTOR:
                nc.vector.tensor_copy(tour[b][:, t, :], picked)
            else:
                nc.scalar.activation(tour[b][:, t, :], picked, ACT.Copy)

        def pick_product(prod, b, t):
            nc.vector.tensor_tensor(prod, h[b, t][:].indirect(pos_sb[SAIL][:]), tour[b][:, t, :], ALU.mult)

        def pick_docks(lo, hi, on_vector):
            dock = keep.tile([P, PACK, hi - lo], F32, name=f"dock1_{lo}", tag="late" if lo else f"prod0{HOLD}")
            for t in range(PACK):
                picked = h[1, t][:].indirect(places(DOCK, lo, hi))
                if t < on_vector:
                    nc.vector.tensor_copy(dock[:, t, :], picked)
                else:
                    nc.scalar.activation(dock[:, t, :], picked, ACT.Copy)
            size = keep.tile([P, PACK, hi - lo], F32, name=f"size{lo}", tag="z_t" if lo else "size", align_bytes=64)
            nc.scalar.activation(size[:], dock[:], ACT.Abs)
            return size

        def quantise(grouped, name):
            width = grouped.shape[1] // PACK
            codes = keep.tile([P, width], U32, name=f"{name}_codes", align_bytes=64)
            scales = keep.tile([P, width], U8, name=f"{name}_sc", align_bytes=64)
            nc.vector.quantize_mx(out=codes[:].bitcast(E4M3), scales=scales[:], in_=grouped)
            return codes, scales

        def quantise_z(dock, prod, b, lo, hi):
            grouped = keep.tile([P, hi - lo, PACK], BF16, name=f"z_grouped{b}_{lo}", align_bytes=64)
            nc.vector.tensor_tensor(
                grouped[:].rearrange("p (c i) t -> p c t i", i=2),
                dock.rearrange("p t (c i) -> p c t i", i=2),
                prod.rearrange("p t (c i) -> p c t i", i=2),
                ALU.add,
            )
            return quantise(grouped[:].rearrange("p m t -> p (m t)"), f"z{b}_{lo}")

        h = {}
        e = {(b, t): features("e", b, t) for b in range(PASSES) for t in range(PACK)}
        tour = [keep.tile([P, PACK, M], F32, name="tour0")]
        for t in range(PACK):
            pick_tour(e[0, t], 0, t)
        quantise_w1(0)
        target_sb = big([P, N_TILES, M], F32, "target_sb", 0)
        nc.sync.dma_start(target_sb[:], target.rearrange("(t p) m -> p t m", p=P))
        quantise_w1(1)
        tour.append(big([P, PACK, M], F32, "tour1", 1))
        for t in range(PACK):
            h[0, t] = features("h", 0, t)
        for t in range(PACK):
            pick_tour(e[1, t], 1, t)
        w4_w = ring.tile([P, PASSES, N], I32, name="w4_w", tag="w1_grouped", bufs=1, align_bytes=64)
        nc.sync.dma_start(w4_w[:], w4_words.rearrange("a p c i -> p a (c i)").bitcast(I32))
        w4_sc = w1_codes[0][:, 0, : N // 4].bitcast(U8)
        for q in range(QUADS):
            nc.sync.dma_start(
                w1_codes[0][32 * q : 32 * q + 8, 0, : N // 4].bitcast(I32),
                w4_scales[:, 4 * q : 4 * q + 4, :].bitcast(I32),
            )
        h[1, 0] = features("h", 1, 0)
        z_t = keep.tile([P, M_TILES * PASS], BF16, name="z_t", tag="z_t", align_bytes=64)
        for j in range(PACK):
            if j + 1 < PACK:
                h[1, j + 1] = features("h", 1, j + 1)
            dock = keep.tile([P, M], F32, name=f"dock0{j}")
            nc.vector.tensor_copy(dock[:], h[0, j][:].indirect(pos_sb[DOCK][:]))
            prod = keep.tile([P, M], F32, name=f"prod0{j}", tag=f"prod0{j}")
            pick_product(prod[:], 0, j)
            lift = keep.tile([P, M], F32, name=f"lift{j}")
            nc.vector.tensor_scalar(lift[:], dock[:], -2.0, 0.0, ALU.mult, ALU.max)
            turned = sums.tile([P, M_TILES, P], F32, name="acc")
            for mt in range(M_TILES):
                cols = slice(mt * P, (mt + 1) * P)
                terms = (dock[:, cols], lift[:, cols], prod[:, cols])
                for i, term in enumerate(terms):
                    nc.tensor.matmul(
                        turned[:, mt, :], term, ident[:], start=(i == 0), stop=(i == 2), is_transpose=True
                    )
            dst = z_t[:].rearrange("p (t u j q e) -> p t u j q e", u=2, j=PACK, q=32, e=2)[:, :, :, j, :, :]
            nc.scalar.copy(dst, turned[:].rearrange("p t (q u e) -> p t u q e", u=2, e=2))
        early_docks = pick_docks(0, M // 2, on_vector=0)
        grouped0 = keep.tile([P, M * PACK], BF16, name="z_grouped0", align_bytes=64)
        for pair in range(M_TILES // 2):
            back = sums.tile([P, 2, 2, P], F32, name="acc")
            for i in range(2):
                words = z_t[:, (2 * pair + i) * PASS : (2 * pair + i + 1) * PASS].bitcast(F32)
                for u in range(2):
                    nc.tensor.transpose(back[:, i, u, :], words[:, u * P : (u + 1) * P], ident[:])
            nc.scalar.copy(
                grouped0[:, 2 * pair * PASS : 2 * (pair + 1) * PASS]
                .bitcast(F32)
                .rearrange("p (t m u) -> p t m u", t=2, u=2),
                back[:].rearrange("p t u m -> p t m u"),
            )
        z0 = quantise(grouped0[:], "z0")

        def scores(lo, hi, z1):
            width = hi - lo
            per_bank = BANK // width
            banks = []
            for first in range(0, N_TILES, per_bank):
                y = sums.tile([P, per_bank, width], F32, name="acc")
                for b in range(PASSES):
                    codes, scales = (z0[0][:, lo:hi], z0[1][:, lo:hi]) if b == 0 else (z1[0][:], z1[1][:])
                    for i in range(per_bank):
                        cols = slice((first + i) * P, (first + i + 1) * P)
                        nc.tensor.matmul_mx(
                            out=y[:, i, :],
                            lhsT=w4_w[:, b, cols].bitcast(E4M3),
                            lhsT_scale=w4_sc[4 * b :, cols],
                            rhs=codes.bitcast(E4M3),
                            rhs_scale=scales,
                            start=(b == 0 and i == 0),
                            stop=(b == PASSES - 1 and i == per_bank - 1),
                        )
                banks.append((y, first, per_bank))
            return banks

        def residual(y, first, count, lo, hi):
            res = ring.tile([P, count, hi - lo], F32, name="res", bufs=6)
            sq = ring.tile([P, count, hi - lo], F32, name="sq", bufs=6)
            nc.vector.tensor_tensor(res[:], target_sb[:, first : first + count, lo:hi], y, ALU.subtract)
            nc.scalar.activation(sq[:], res[:], ACT.Square)
            return res, sq, first, count, lo, hi

        def finish(res, sq, first, count, lo, hi):
            engine = nc.gpsimd if (lo, first) == (0, 0) else nc.vector
            engine.tensor_tensor(sq[:], sq[:], res[:], ALU.mult)
            nc.sync.dma_start(out.rearrange("(t p) m -> p t m", p=P)[:, first : first + count, lo:hi], sq[:])

        prod1 = keep.tile([P, PACK, M], F32, name="prod1")
        for t in range(PACK):
            pick_product(prod1[:, t, :], 1, t)
        late_docks = pick_docks(M // 2, M, on_vector=LATE_ON_VECTOR)
        banks, squared = [], []
        for lo, hi in PIECES:
            docks = early_docks[:] if lo < M // 2 else late_docks[:, :, lo - M // 2 : hi - M // 2]
            z1 = quantise_z(docks, prod1[:, :, lo:hi], 1, lo, hi)
            for job in squared:
                finish(*job)
            squared = [residual(*job) for job in banks]
            banks = [(y[:], first, count, lo, hi) for y, first, count in scores(lo, hi, z1)]
        for job in squared:
            finish(*job)
        last = [residual(y[:, i : i + 1, :], first + i, 1, lo, hi) for y, first, count, lo, hi in banks for i in range(count)]
        for job in last:
            finish(*job)
